import numpy as np, ml_dtypes
CORES = [6,15,38,47]
N = 4
BF = ml_dtypes.bfloat16
W, V, L, S, T, E = 4096, 1024, 256, 16, 6, 1
def parts(rng):
    x = (64 * rng.random((N, 8, 16, W)) * (0.5 + 0.5 * rng.random((N, 8, 1, W)))).astype(np.int64)
    im = (64 * rng.random((N, 8, 16, V)) * (0.25 + 0.75 * rng.random((N, 8, 1, V)))).astype(np.int64)
    z = (64 * rng.random((N, 8, 16, 2, L)) * (0.5 + 0.5 * rng.random((N, 8, 1, 2, L)))).astype(np.int64)
    b = rng.integers(0, W, (N, 8, 16, V)); q = np.minimum((8 * rng.random((N, 8, 16, V)) ** 0.6).astype(np.int64), 7)
    return x, im, b, q, z, rng.integers(1, 4096, (N, 8, 16))
def pack(x, im, b, q, z, w):
    return {"geno": x.reshape(N, 128, W).astype(np.float32).astype(BF), "immun": im.reshape(N, 128, V).astype(np.float32).astype(BF),
            "bank": (b + W * q).reshape(N, 128, V).astype(np.int32), "bites": z.reshape(N, 128, 2 * L).astype(np.float32).astype(BF), "wt": w.reshape(N, 128, 1).astype(np.int32)}
def first(z, w):
    u = np.sum(w[:, :, :, None] * z[:, :, :, 0], axis=2) & 4095
    return ((u * u >> 5) + 37 * u) & (V - 1)
def setup_inputs(rng):
    return pack(*parts(rng))
def setup_inputs_corners(rng):
    x, im, b, q, z, w = parts(rng); w[:, :, 0] = 4095; w[:, :, 1] = 2048
    kind = rng.integers(0, 4, (N, 8, 1, V)); im = np.where(kind == 0, 0, np.where(kind == 1, 63, im))
    mode = rng.integers(0, 7, (N, 8, 1, V)); pos = np.argsort(rng.random((N, 8, 16, V)), axis=2); near = E - 1 + rng.integers(0, 3, q.shape)
    q = np.where(mode == 5, q[:, :, :1], q); q = np.where(mode == 4, near, q); q = np.where(mode == 3, 7 * (pos < 2), q)
    q = np.where(mode == 2, 7 * (pos < 1), q); q = np.where(mode == 1, 0, q); q = np.where(mode == 0, 7, q)
    edge = rng.integers(0, 4, (N, 8, 1, V)); b = np.where(edge == 0, (W - 1) * rng.integers(0, 2, b.shape), b); b = np.where(edge == 1, b[:, :, :1], b)
    z[:, :, :, 0, 4:L - 1] = np.maximum(z[:, :, :, 0, 4:L - 1], 1)
    z[:, :, :, :, 0] = 0; z[:, :, :, :, 1] = 63; z[:, :, :, :, 2] = 0; z[:, :, 1, :, 2] = 1; z[:, :, :, :, L - 1] = 0; z[:, :, 0, :, L - 1] = 1
    v = first(z, w); n = L // 2; m = L // 8
    for a in range(N):
        for g in range(8):
            lanes = (4 + rng.permutation(L - 5))[:n]; zz = z[a, g, :, 0][:, lanes]
            po = np.argsort(rng.random((16, n)), axis=0); cnt = 8 + np.arange(n) % 3
            im[a, g][:, v[a, g, lanes]] = zz - (po < cnt)
            own = lanes[:m]; k = rng.integers(0, 16, m); h = v[a, g, own]
            b[a, g, k, h] = S * own; q[a, g, k, h] = 7
            x[a, g][:, S * own] = np.where(zz[:, :m] < 32, 63, 0)
    return pack(x, im, b, q, z, w)
def setup_inputs_crowd(rng):
    x, im, b, q, z, w = parts(rng); w = np.repeat(rng.integers(1, 4096, (N, 8, 1)), 16, axis=2)
    for a in range(N):
        for g in range(8):
            for c in range(2):
                n = int(rng.choice(np.array([1, 2, 5, 17, 30])))
                if g == a % 8 and c == 0: n = 1
                if g == (a + 3) % 8 and c == 0: continue
                base = z[a, g, :, c, :n].copy()[:, rng.integers(0, n, L)]
                z[a, g, :, c] = np.take_along_axis(base, np.argsort(rng.random((16, L)), axis=0), 0)
        g = (a + 3) % 8; w[a, g] = rng.integers(1, 4096, 16); w[a, g, 0] = 1; w[a, g, 15] = 64
        u = rng.permutation(4096); u = u[np.unique(((u * u >> 5) + 37 * u) & (V - 1), return_index=True)[1]]
        need = (rng.permutation(u)[:L] - np.sum(w[a, g, 1:15, None] * z[a, g, 1:15, 0], axis=0)) & 4095
        z[a, g, 0, 0] = need & 63; z[a, g, 15, 0] = need >> 6
    return pack(x, im, b, q, z, w)
def setup_inputs_ends(rng):
    def rec(n):
        k = rng.integers(0, 3, (N, 8, 1, n)); return 63 * np.where(k == 2, rng.integers(0, 2, (N, 8, 16, n)), k)
    x = rec(W); im = rec(V); z = rec(2 * L).reshape(N, 8, 16, 2, L); w = np.where(rng.integers(0, 2, (N, 8, 16)) == 1, 4095, 1); w[N - 1, 7] = 4095
    x[:, 1::2, :, W - 1] = 0; x[:, ::2, :, W - 1] = 63 * rng.integers(0, 2, (N, 4, 16))
    nz = rng.integers(0, 8, (8, 1, L)) * rng.integers(0, 2, (8, 1, L)); nz[:, :, 0] = 0; nz[:, :, L - 1] = 0
    nz[0, 0, ::2] = 0; nz[0, 0, 1] = 1; nz[0, 0, L - 1] = 0
    z[N - 1, :, :, 0] = 63 * (np.argsort(rng.random((8, 16, L)), axis=1) >= nz)
    z[1, :, :, 0] = 63 * (np.argsort(rng.random((8, 16, L)), axis=1) >= rng.integers(0, 8, (8, 1, L)))
    v = first(z, w); r = np.arange(16)[None, None, :, None]; mode = rng.integers(0, 5, (N, 8, 1, V))
    fl = (mode == 0) | ((mode == 1) & (r >= 14)) | ((mode == 2) & ((r == 0) | (r == 15))) | ((mode == 4) & (rng.random((N, 8, 16, V)) < 0.5))
    anyb = (rng.random((N, 8, 1, V)) < 0.5) & fl
    for g in range(8):
        for a in (1, N - 1):
            h = v[a, g]; fl[a, g, 14:][:, h] = True; anyb[a, g][:, h] = False; im[a, g][:, h] = 0
        im[0, g][:, v[0, g]] = 63
    im[N - 1, 0][:, v[N - 1, 0, 1]] = 63
    woke = 16 * L - 2 * int(np.sum(v[N - 1, 0] == v[N - 1, 0, 1])); assert woke > 15 * L and woke & (V - 1) != 0
    b = np.where(fl, np.where(anyb, rng.integers(0, W, fl.shape), W - 1), 0); q = 7 * fl
    for g, ks in ((1, (2, 5, 9)), (3, (0, 1, 15)), (5, (13, 14, 15))):
        h = v[N - 1, g, 0]; x[N - 1, g, :, W - 2] = 0; x[N - 1, g, rng.integers(0, 16), W - 2] = 1
        b[N - 1, g, :, h] = 0; q[N - 1, g, :, h] = 0
        for k, c in zip(ks, (W - 2, W - 2, W - 1)):
            b[N - 1, g, k, h] = c; q[N - 1, g, k, h] = 7
    return pack(x, im, b, q, z, w)
def setup_inputs_spread(rng):
    x, im, b, q, z, w = parts(rng)
    def pw(*s): return rng.random(s) ** np.exp2(rng.integers(-2, 4, s[:2] + (1,) + s[3:]))
    x = np.minimum((64 * pw(N, 8, 16, W)).astype(np.int64), 63); im = np.minimum((64 * pw(N, 8, 16, V)).astype(np.int64), 63)
    z = np.minimum((64 * pw(N, 8, 16, 2, L)).astype(np.int64), 63); b = np.minimum((W * pw(N, 8, 16, V)).astype(np.int64), W - 1)
    q = np.minimum((8 * rng.random((N, 8, 16, V)) ** np.exp2(rng.integers(-2, 2, (N, 8, 1, V)))).astype(np.int64), 7)
    w = np.minimum(np.exp2(12 * rng.random((N, 8, 16))).astype(np.int64), 4095)
    return pack(x, im, b, q, z, np.maximum(w, 1))
def setup_inputs_ties(rng):
    lv = rng.integers(0, 3, (N, 8, 1, W)); x = lv + rng.integers(0, 3, (N, 8, 16, W)); im = rng.integers(0, 3, (N, 8, 16, V))
    z = rng.integers(0, 3, (N, 8, 1, 2, L)) + rng.integers(0, 3, (N, 8, 16, 2, L)); w = rng.integers(1, 4096, (N, 8, 16)); b = rng.integers(0, W, (N, 8, 16, V))
    q = np.where(rng.random((N, 8, 16, V)) < 0.5, rng.integers(0, 8, (N, 8, 1, V)), rng.integers(4, 8, (N, 8, 1, V)))
    x[:, ::2, :, W // 2:] = x[:, ::2, :, :W // 2]; b[:, :, 8:, ::2] = b[:, :, :8, ::2]
    z[:, :, :, 0, ::4] = np.take_along_axis(x, rng.integers(0, W, (N, 8, 1, L // 4)), 3)
    x[:, 1::2] += 59; im[:, 1::2] += 59; z[:, 1::2] += 59
    r = np.arange(16)[:, None]; x[:, 2] = (r + np.arange(W)) % 3; z[:, 2, :, 0] = (r + np.arange(L)) % 3; im[:, 2] = 0
    same = ((4, 0, [15]), (6, L // 2, [2, 15]), (7, L - 1, [15])); cz = rng.integers(0, W, (N, 8))
    for a in range(N):
        for g, j, ks in same:
            e = 59 * (g % 2) + rng.integers(1, 3, 16); z[a, g, :, 0, j] = e; x[a, g, :, cz[a, g]] = e
    v = first(z, w)
    for a in range(N):
        for j in range(3):
            h = v[a, 2, j]; q[a, 2, :, h] = 0; q[a, 2, 3, h] = 7; q[a, 2, 12, h] = 7
            b[a, 2, 3, h] = 3 * rng.integers(0, W // 3) + (j + 1) % 3; b[a, 2, 12, h] = 3 * rng.integers(0, W // 3) + (j + 2) % 3
        for g, j, ks in same:
            h = v[a, g, j]; im[a, g, :, h] = 0; q[a, g, :, h] = 0; b[a, g, 15, h] = cz[a, g]
            for k in ks: q[a, g, k, h] = 7
    return pack(x, im, b, q, z, w)
def check_inputs(d):
    bad = []
    for k, lo, hi in (("geno", 0, 63), ("immun", 0, 63), ("bank", 0, 8 * W - 1), ("bites", 0, 63), ("wt", 1, 4095)):
        a = np.asarray(d[k]).astype(np.float64)
        if not np.all((a >= lo) & (a <= hi)): bad.append("range of " + k)
        elif np.any(a != np.floor(a)): bad.append("whole numbers of " + k)
    return bad
def beats(a, c):
    return (np.sum(a > c, axis=2) >= 9).astype(np.int64)
def reference(geno, immun, bank, bites, wt):
    X = geno.astype(np.float32).astype(np.int64).reshape(N, 8, 16, W); im = immun.astype(np.float32).astype(np.int64).reshape(N, 8, 16, V)
    bk = bank.astype(np.int64).reshape(N, 8, 16, V); z = bites.astype(np.float32).astype(np.int64).reshape(N, 8, 16, 2, L); w = wt.astype(np.int64).reshape(N, 8, 16, 1)
    todo = [z[:, :, :, 0], np.roll(z[:, :, :, 1], 1, axis=0)]
    A = np.zeros(N, np.int64); row = np.arange(16)[None, None, :, None]; lane = np.arange(L)[None, None, None, :]
    for t in range(T):
        s = todo[t]
        u = np.sum(w * s, axis=2) & 4095; v = ((u * u >> 5) + 37 * u + A[:, None, None]) & (V - 1)
        e = np.take_along_axis(bk, v[:, :, None, :], 3); b = e & (W - 1); q = e // W
        iv = np.take_along_axis(im, v[:, :, None, :], 3)
        c = np.take_along_axis(X, b.reshape(N, 8, 1, 16 * L), 3).reshape(N, 8, 16, 16, L)
        D = np.sum(np.abs(c - s[:, :, :, None, :]), axis=2)
        sick = np.sum(s > iv, axis=2) >= 9
        key = np.where((q >= t + E) & sick[:, :, None, :], D * 16 + 15 - row, -1)
        k1 = np.argmax(key, axis=2); h1 = (np.max(key, axis=2) >= 0).astype(np.int64)
        key = np.where(row == k1[:, :, None, :], -1, key)
        k2 = np.argmax(key, axis=2); h2 = (np.max(key, axis=2) >= 0).astype(np.int64)
        a1 = np.take_along_axis(c, k1[:, :, None, None, :], 3)[:, :, :, 0]; a2 = np.take_along_axis(c, k2[:, :, None, None, :], 3)[:, :, :, 0]
        n0 = h1 * beats(a1, s) + h2 * beats(a2, s); n1 = beats(s, a1) + h2 * beats(a2, a1); n2 = beats(s, a2) + beats(a1, a2)
        o = np.argsort(np.stack([n0 * 4, np.where(h1 == 1, n1 * 4 + 1, 97), np.where(h2 == 1, n2 * 4 + 2, 98)]), axis=0)
        st = np.stack([s, a1, a2]); second = np.where(h1 == 1, o[1], 0)
        f = np.take_along_axis(st, o[0][None, :, :, None, :], 0)[0]; m = np.take_along_axis(st, second[None, :, :, None, :], 0)[0]
        todo.append(np.roll(np.where((u[:, :, None, :] >> (row & 7)) & 1 == 1, f, m), 2, axis=0))
        wake = ((row == k1[:, :, None, :]) & (h1[:, :, None, :] == 1)) | ((row == k2[:, :, None, :]) & (h2[:, :, None, :] == 1))
        q = np.where(wake, 0, q); slot = np.argmin(q * 16 + row, axis=2)
        e = np.where(row == slot[:, :, None, :], S * lane + t + W * (8 + t), b + W * q); iv = np.maximum(iv - 1, f)
        for a in range(N):
            for g in range(8):
                hv, fi = np.unique(v[a, g], return_index=True)
                bk[a, g][:, hv] = e[a, g][:, fi]; im[a, g][:, hv] = iv[a, g][:, fi]
        X[:, :, :, t::S] = s
        A = np.sum(h1 + h2, axis=(1, 2))
    return {"ybank": bk.reshape(N, 128, V).astype(np.float32), "yimm": im.reshape(N, 128, V).astype(np.float32).astype(BF), "ygeno": X.reshape(N, 128, W).astype(np.float32).astype(BF)}

@@ -1,0 +1,596 @@
+from concourse.mybir import dt, AluOpType, AxisListType, ActivationFunctionType
+
+OP = AluOpType
+AF = ActivationFunctionType
+BIG = 1048576.0
+STEPS = 6
+TILES = {
+    "bt": (256, "bfloat16", 1), "geno_s": (4096, "bfloat16", 1), "bk": (1024, "int32", 1), "im0": (1024, "bfloat16", 1),
+    "wti": (1, "int32", 1), "btab": (1280, "float32", 1), "qtab": (1280, "float32", 1), "itab": (1280, "float32", 1),
+    "cb": (256, "bfloat16", 4),
+    "CZ": (4880, "bfloat16", 6), "mx": (4096, "bfloat16", 2),
+    "bki": (1024, "int32", 1), "qki": (1024, "int32", 1),
+    "yb": (1024, "float32", 1), "yi": (1024, "bfloat16", 1),
+    "pI": (8, "int32", 1), "pM": (8, "int32", 1), "pG": (8, "int32", 1), "pf": (32, "float32", 1), "wf": (16, "float32", 1), "wi2": (16, "int32", 1),
+    "ic": (256, "float32", 1), "icg": (128, "float32", 1), "ir": (256, "float32", 1),
+    "I": (128, "bfloat16", 1), "nI": (128, "bfloat16", 1), "IB": (128, "bfloat16", 1), "I16": (128, "bfloat16", 1), "Is": (128, "bfloat16", 1),
+    "Gf": (128, "float32", 1), "Gs": (128, "float32", 1), "SC": (128, "float32", 1), "wSh": (128, "bfloat16", 1), "wSl": (128, "bfloat16", 1),
+    "Gm": (16, "bfloat16", 1), "Gmf": (8, "float32", 1), "G64": (16, "bfloat16", 1), "G32": (16, "bfloat16", 1),
+    "EB": (144, "bfloat16", 1), "wEh": (144, "bfloat16", 1), "wEl": (144, "bfloat16", 1), "RB": (240, "bfloat16", 1),
+    "mO": (256, "float32", 1), "C16": (256, "bfloat16", 1), "ones": (128, "bfloat16", 1), "kidx": (256, "int32", 1),
+    "bci": (16, "int32", 1), "bc": (16, "uint16", 1), "lnO": (16, "float32", 1), "lnD": (16, "float32", 1), "lnH": (16, "float32", 1), "C48": (48, "float32", 1),
+    "ln32": (32, "float32", 1), "ls32": (32, "float32", 1), "tp32": (32, "float32", 1), "ba32": (32, "float32", 1), "sp32": (32, "float32", 1),
+    "NEW": (256, "float32", 2),
+    "ui": (16, "int32", 2), "u": (16, "int32", 2), "sq": (16, "int32", 2), "sh": (16, "int32", 2), "u37": (16, "int32", 2), "base": (16, "int32", 2),
+    "vb": (16, "int32", 2), "dd": (16, "float32", 2), "b1": (16, "float32", 2), "b2": (16, "float32", 2),
+    "Zf": (256, "float32", 2), "junk": (256, "bfloat16", 8), "c1": (16, "float32", 2), "c2": (16, "float32", 2),
+    "bti": (256, "int32", 2), "bit": (256, "int32", 2),
+    "vA": (16, "int32", 2), "v": (16, "int32", 2), "vl": (16, "uint16", 2), "dup": (16, "float32", 2), "dv": (16, "float32", 2), "dw": (16, "float32", 2),
+    "wo": (16, "float32", 2), "wl": (16, "uint16", 2),
+    "boff": (256, "uint16", 2), "db": (256, "float32", 2), "qg": (256, "bfloat16", 2), "ig": (256, "bfloat16", 2), "im1": (256, "float32", 2),
+    "fl": (256, "bfloat16", 2), "gt": (256, "bfloat16", 2), "qks": (128, "float32", 2), "q1": (128, "float32", 2), "q2": (64, "float32", 2), "q3": (32, "float32", 2),
+    "m0": (16, "float32", 2), "n1": (32, "float32", 2), "nsB": (32, "float32", 2), "sk": (16, "float32", 2), "ac": (16, "bfloat16", 2), "A": (8, "float32", 2),
+    "keys": (256, "float32", 2), "h1": (128, "float32", 1), "l1": (128, "float32", 1), "h2": (64, "float32", 1), "mn2": (64, "float32", 1), "ml2": (64, "float32", 1), "l2": (64, "float32", 1),
+    "h3": (32, "float32", 1), "mn3": (32, "float32", 1), "ml3": (32, "float32", 1), "l3": (32, "float32", 1), "mn4": (16, "float32", 1), "ml4": (16, "float32", 1),
+    "HL": (32, "float32", 2), "flg": (32, "float32", 2), "HI": (32, "int32", 2), "HA": (32, "int32", 2), "KM": (32, "float32", 2), "thr": (16, "float32", 2),
+    "kx": (16, "float32", 2), "sm": (16, "float32", 2), "si": (16, "int32", 2), "sl": (16, "int32", 2), "awsl": (512, "bfloat16", 2),
+    "tb": (256, "float32", 1), "t1": (256, "bfloat16", 1), "t2": (256, "bfloat16", 1), "t3": (256, "float32", 1),
+    "Y": (256, "bfloat16", 2), "mz": (32, "float32", 1), "tm": (32, "float32", 1), "bm": (32, "float32", 1), "of": (32, "float32", 1), "al": (32, "uint16", 2),
+    "SG": (1536, "bfloat16", 1), "TH": (96, "float32", 1), "KK": (48, "float32", 1), "KL": (48, "float32", 1), "mna": (16, "float32", 1), "mxa": (16, "float32", 1), "tta": (16, "float32", 1),
+    "FM": (32, "float32", 1), "FI": (32, "int32", 1), "FA": (32, "int32", 1), "fml": (32, "uint16", 2), "fmb": (512, "bfloat16", 1), "ff": (256, "float32", 1), "tX": (256, "bfloat16", 1),
+}
+BYTES = {"float32": 4, "int32": 4, "bfloat16": 2, "uint16": 2}
+PLACE = {}
+_size = {d: 0 for d in BYTES}
+for _n, (_w, _d, _c) in TILES.items():
+    _p = (_w + 15) // 16 * 16
+    PLACE[_n] = (_size[_d], _p)
+    _size[_d] += _p * _c
+BUF = {"float32": "bigf", "int32": "bigi", "bfloat16": "bigb", "uint16": "bigu"}
+SCRATCH = {BUF[_d]: ("sbuf", [128, _size[_d]], _d) for _d in BYTES}
+for _k in range(8):
+    SCRATCH["P%d" % _k] = ("psum", [128, 512], "float32")
+LOADS = ["bites", "next", "wt", "bank", "immun", "geno"]
+STORES = ["sg", "sb0", "sb1", "si0", "si1"]
+SEMAPHORES = ["qv", "qs", "qp", "qg", "rl"] + ["arr%d" % t for t in range(1, STEPS)] + ["ld_" + n for n in LOADS] + ["st_" + n for n in STORES]
+
+
+BIAS = {'ic': -8, 'qtab': -7, 'qki': -8, 'P4awsl': -1, 'v': 16, 'ln32': 2, 'bci': 9, 'thr': -13, 'I': 18, 'P6nI': -10, 'SC': 5, 'KL': 19, 'mO': -21, 'ir': 4, 'ba32': -5, 'tb': -2, 'RB': -1, 'ls32': 14, 'HL': -21, 'mn4': -3, 'P2wEh': 3, 'ac': 7, 'geno_s': -18, 'ml3': -2, 'db': -3, 'Gm': -2, 'P1CZ': 9, 'NEW': 2, 'sm': -1, 'lnH': -1, 'outsi1': 9, 'wti': -13, 'P1fl': 3, 'P4qtab': -1, 'vA': 8}
+COST = {"us": 0.00083 * 1.25, "ps": 0.00071 * 1.25, "gather": 1.56, "scatter": 3.8, "wake": 0.08, "link": 4.0}
+LOOK = 0.3
+
+
+def list_schedule(n, que, cost, succ, need, prio):
+    need = list(need)
+    when = [0.0] * n
+    free, ready, nxt = {}, {}, {}
+    order = []
+    for i in range(n):
+        if need[i] == 0:
+            ready.setdefault(que[i], []).append(i)
+    dirty = set(ready)
+    end = 0.0
+    while len(order) < n:
+        for q in dirty:
+            lst = ready.get(q)
+            if not lst:
+                nxt.pop(q, None)
+                continue
+            f = free.get(q, 0.0)
+            st = max(f, min(when[i] for i in lst))
+            c = -1
+            for i in lst:
+                if when[i] <= st + 1e-9 and (c < 0 or prio[i] > prio[c]):
+                    c = i
+            if cost[c] > LOOK:
+                lim = st + min(LOOK, 0.5 * cost[c])
+                b = c
+                for i in lst:
+                    if when[i] <= lim and prio[i] > prio[b]:
+                        b = i
+                c = b
+            nxt[q] = (max(st, when[c]), c)
+        q = min(nxt, key=lambda x: nxt[x][0])
+        st, c = nxt[q]
+        ready[q].remove(c)
+        order.append(c)
+        free[q] = st + cost[c] if q != "n" else 0.0
+        end = max(end, st + cost[c])
+        dirty = {q}
+        for i, l in succ[c]:
+            need[i] -= 1
+            if st + l > when[i]:
+                when[i] = st + l
+            if need[i] == 0:
+                ready.setdefault(que[i], []).append(i)
+                dirty.add(que[i])
+    return order, end
+
+
+def rank_program(g, core, T, topo):
+    rank = T.rank_of(core)
+    if rank is None:
+        return
+    n_ranks = len(T.cores)
+    ops = []
+    last = {}
+    edges = []
+    US, PS = COST["us"], COST["ps"]
+
+    def t_(name, a=0, b=None, c=0, step=1):
+        w, d, copies = TILES[name]
+        if b is None:
+            b = w
+        off, p = PLACE[name]
+        off += p * (c % copies)
+        ap = T[BUF[d]][:, off + a:off + b:step] if step != 1 else T[BUF[d]][:, off + a:off + b]
+        return {"ap": ap, "rg": [(BUF[d], off + a, off + b)], "n": (b - a + step - 1) // step, "by": BYTES[d], "ps": False, "ind": False}
+
+    def p_(k, a, b, step=1, grp=None):
+        ap = T["P%d" % k][:, a:b:step] if step != 1 else T["P%d" % k][:, a:b]
+        return {"ap": ap, "rg": [("P%d" % k, 0, 512)], "n": (b - a + step - 1) // step, "by": 4, "ps": True, "ind": False, "grp": grp}
+
+    def ind(win, off):
+        return {"ap": win["ap"].indirect(off["ap"]), "rg": win["rg"] + off["rg"], "win": win["rg"], "off": off["rg"], "n": 16 * off["n"], "by": win["by"], "ps": False, "ind": True}
+
+    starts = {d: sorted((PLACE[x][0], x) for x in TILES if TILES[x][1] == d) for d in BUF}
+    dtype_of = {BUF[d]: d for d in BUF}
+
+    def name_of(region):
+        if region[0] not in dtype_of:
+            return region[0]
+        return [x for o, x in starts[dtype_of[region[0]]] if o <= region[1]][-1]
+
+    def add(q, cost, emit, R, W, sem, inc, grp=None, role=None, extra=()):
+        i = len(ops)
+        ed = {}
+        acc = [(r, False) for r in R] + [(r, True) for r in W]
+        for (buf, a, b), wr in acc:
+            ps = buf.startswith("P") and len(buf) == 2
+            for (a2, b2, j, wr2, q2, grp2, role2) in last.get(buf, []):
+                if a2 >= b or b2 <= a or j == i:
+                    continue
+                if ps:
+                    if q2 == q:
+                        if q == "p" and not (grp is not None and grp == grp2 and role == "mid" and role2 == "mid"):
+                            ed.setdefault(j, 0)
+                    else:
+                        ed[j] = 1
+                elif wr or wr2:
+                    ed[j] = 1
+        for j in extra:
+            ed[j] = 1
+        for (buf, a, b), wr in acc:
+            ps = buf.startswith("P") and len(buf) == 2
+            lst = last.setdefault(buf, [])
+            if wr and not ps:
+                lst[:] = [x for x in lst if not (x[0] >= a and x[1] <= b and x[2] != i)]
+            lst.append((a, b, i, wr, q, grp, role))
+            if ps and len(lst) > 200:
+                del lst[:80]
+        tag = name_of(W[0]) if W else q
+        if tag[0] == "P" and R:
+            tag += name_of(R[0])
+        ops.append({"q": q, "cost": cost, "emit": emit, "sem": sem, "inc": inc, "tag": tag})
+        edges.append(ed)
+        return i
+
+    def rgs(*xs):
+        out = []
+        for x in xs:
+            if isinstance(x, dict):
+                out += x["rg"]
+        return out
+
+    def raw(x):
+        return x["ap"] if isinstance(x, dict) else x
+
+    def vcost(n, mode, xs):
+        if any(x["ind"] for x in xs[1:]):
+            return 0.05 + n * COST["gather"] * US
+        if xs[0]["ind"]:
+            return 0.05 + n * COST["scatter"] * US
+        if mode == "tt":
+            c = n * (1 if any(x["ps"] for x in xs) else 2)
+        else:
+            c = n * (0.5 if all(x["by"] == 2 for x in xs) else 1)
+        return max(64, c) * US
+
+    def outrg(out):
+        return (out["off"], out["win"]) if out["ind"] else ([], out["rg"])
+
+    def tt(out, a, b, op):
+        r, w = outrg(out)
+        n = out["n"]
+        return add("v", vcost(n, "tt", [out, a, b]), lambda: g.vector.tensor_tensor(raw(out), raw(a), raw(b), op), rgs(a, b) + r, w, "qv", 1)
+
+    def ts(out, a, s1, s2, o1, o2=None):
+        r, w = outrg(out)
+        f = (lambda: g.vector.tensor_scalar(raw(out), raw(a), raw(s1), raw(s2), o1)) if o2 is None else (lambda: g.vector.tensor_scalar(raw(out), raw(a), raw(s1), raw(s2), o1, o2))
+        return add("v", vcost(out["n"], "ts", [out, a]), f, rgs(a, s1, s2) + r, w, "qv", 1)
+
+    def cp(out, a):
+        r, w = outrg(out)
+        return add("v", vcost(out["n"], "ts", [out, a]), lambda: g.vector.tensor_copy(raw(out), raw(a)), rgs(a) + r, w, "qv", 1)
+
+    def ms(out, val):
+        return add("v", max(64, out["n"]) * US, lambda: g.vector.memset(raw(out), val), [], out["rg"], "qv", 1)
+
+    def red(out, a):
+        return add("v", 64 * US, lambda: g.vector.tensor_reduce(raw(out), raw(a), AxisListType.X, OP.add), rgs(a), out["rg"], "qv", 1)
+
+    def act(out, a, fn, bias=0.0, scale=1.0, acc=None):
+        c = 0.065 + a["n"] * COST["gather"] * US if a["ind"] else max(64, a["n"]) * US
+        w = out["rg"] + (acc["rg"] if acc else [])
+        if acc:
+            c += 0.02
+            f = lambda: g.scalar.activation(raw(out), raw(a), fn, bias=raw(bias), scale=scale, accum_out=raw(acc))
+        elif isinstance(bias, float) and bias == 0.0:
+            f = (lambda: g.scalar.activation(raw(out), raw(a), fn, scale=raw(scale))) if scale != 1.0 else (lambda: g.scalar.activation(raw(out), raw(a), fn))
+        else:
+            f = lambda: g.scalar.activation(raw(out), raw(a), fn, bias=raw(bias), scale=scale)
+        return add("s", c, f, rgs(a, bias, scale), w, "qs", 1)
+
+    def mm(out, lhsT, rhs, start, stop, grp=None, role=None, f32=False):
+        c = max(64, rhs["n"]) * PS * (4 if f32 else 1)
+        return add("p", c, lambda: g.tensor.matmul(raw(out), raw(lhsT), raw(rhs), start, stop), rgs(lhsT, rhs), out["rg"], "qp", 1, grp=grp, role=role)
+
+    def iota(out, pattern, base=0, cm=0):
+        small = out["flt"] if "flt" in out else False
+        def f():
+            if small:
+                return g.iota(raw(out), pattern, base, cm, allow_small_or_imprecise_dtypes=True)
+            return g.iota(raw(out), pattern, base, cm)
+        return add("g", 0.13 + 2 * out["n"] * US, f, [], out["rg"], "qg", 1)
+
+    def keep(out, a):
+        return add("g", 0.17 + 2 * out["n"] * US, lambda: g.affine_select(raw(out), raw(a), [[0, out["n"]]], OP.is_ge, 0.0, 0, 0), rgs(a), out["rg"], "qg", 1)
+
+    def flt(x):
+        x["flt"] = True
+        return x
+
+    def load(name, out, q="y"):
+        eng = g.sync if q == "y" else g.scalar
+        src = T.bites[:, 0:256] if name == "bites" else T.bites[:, 256:512] if name == "next" else T[name][:]
+        return add(q, 0.1, lambda: eng.dma_start(raw(out), src), [], out["rg"], "ld_" + name, 16)
+
+    def store(tag, dst, src, q="y"):
+        eng = g.sync if q == "y" else g.scalar
+        return add(q, 0.1, lambda: eng.dma_start(dst, raw(src)), src["rg"], [("out" + tag, 0, 1)], "st_" + tag, 16)
+
+    lag = {}
+
+    for name, dst, tm in (("bites", t_("CZ", 4112, 4368, 0), 2.6), ("wt", t_("wti"), 2.5), ("bank", t_("bk"), 4.5), ("immun", t_("im0"), 5.0), ("next", t_("bt"), 4.0), ("geno", t_("geno_s"), 7.0)):
+        i = load(name, dst, "s" if name in ("wt", "immun", "next") else "y")
+        lag[i] = tm
+
+    def send(src, t, dst_rank):
+        dst = T.cores[dst_rank]
+        rid, pid, _se = topo.addr(dst)
+        m = topo.mask(core, dst)
+        eng = len(topo.engines(core, dst))
+        out = t_("CZ", 4112, 4368, t)
+        def f():
+            return g.remote_dma(raw(out), raw(src), T.sem["arr%d" % t], T.sem.rl, pid, rid, m)
+        i = add("g", 0.3, f, src["rg"], [], None, 0)
+        ops[i]["remote"] = eng
+        lag[i] = 0.3
+        j = add("n", 0.0, None, [], out["rg"], "arr%d" % t, eng)
+        ops[j]["proxy"] = i
+        lag[j] = 0.0
+        return i
+
+    iota(t_("pI", 0, 1), [[0, 1]], 0, 1)
+    iota(flt(t_("ic", 0, 128)), [[1, 128]])
+    iota(flt(t_("icg")), [[1, 8], [0, 16]])
+    iota(flt(t_("ir")), [[0, 16], [1, 16]])
+    iota(t_("bci"), [[1, 16]])
+    iota(t_("kidx"), [[0, 16], [1, 16]])
+    iota(flt(t_("lnO")), [[16, 16]])
+    iota(flt(t_("ln32")), [[16, 8], [0, 2], [128, 2]])
+    iota(flt(t_("ls32")), [[0, 8], [1, 2], [0, 2]])
+    send(t_("bt"), 1, (rank + 1) % n_ranks)
+    ts(t_("pM", 0, 1), t_("pI", 0, 1), 15, None, OP.bitwise_and)
+    ts(t_("pG", 0, 1), t_("pI", 0, 1), 4, None, OP.arith_shift_right)
+    P, PM, PG = t_("pf", 0, 1), t_("pf", 8, 9), t_("pf", 16, 17)
+    cp(P, t_("pI", 0, 1))
+    cp(PM, t_("pM", 0, 1))
+    cp(PG, t_("pG", 0, 1))
+    ts(t_("Gmf"), t_("ic", 0, 8), PG, None, OP.is_equal)
+    ms(t_("EB"), 0.0)
+    cp(t_("EB", 15, 128, step=16), t_("Gmf"))
+    ts(t_("wi2", 0, 1), t_("wti"), 4032, None, OP.bitwise_and)
+    ts(t_("wi2", 8, 9), t_("wti"), 63, None, OP.bitwise_and)
+    WH, WL = t_("wf", 0, 1), t_("wf", 8, 9)
+    cp(WH, t_("wi2", 0, 1))
+    cp(WL, t_("wi2", 8, 9))
+    ts(t_("wEh"), t_("EB"), WH, None, OP.mult)
+    ts(t_("wEl"), t_("EB"), WL, None, OP.mult)
+    ts(t_("lnO"), t_("lnO"), PM, None, OP.add)
+    ts(t_("lnD"), t_("lnO"), 1024.0, None, OP.add)
+    ts(t_("lnH"), t_("lnO"), 0.5, None, OP.add)
+    cp(t_("bc"), t_("bci"))
+    ts(t_("mO"), t_("ir"), PM, None, OP.is_equal)
+    ts(t_("Gf"), t_("icg"), PG, None, OP.is_equal)
+    ts(t_("I"), t_("ic", 0, 128), P, None, OP.is_equal)
+    ts(t_("bki"), t_("bk"), 4095, None, OP.bitwise_and)
+    cp(t_("btab", 0, 1024), t_("bki"))
+    ts(t_("qki"), t_("bk"), 12, None, OP.arith_shift_right)
+    cp(t_("qtab", 0, 1024), t_("qki"))
+    act(t_("itab", 0, 1024), t_("im0"), AF.Copy)
+    cp(t_("Gm", 0, 8), t_("Gmf"))
+    ts(t_("G64", 0, 8), t_("Gmf"), 1024.0, None, OP.mult)
+    ts(t_("G32", 0, 8), t_("Gmf"), -512.0, None, OP.mult)
+    ts(t_("nI"), t_("I"), -1.0, None, OP.mult)
+    ts(t_("IB"), t_("I"), BIG, None, OP.mult)
+    ts(t_("I16"), t_("I"), -16.0, None, OP.mult)
+    ts(t_("Is"), t_("I"), 1.0 / 128, None, OP.mult)
+    ts(t_("C16"), t_("ir"), -1.0, 256.0, OP.mult, OP.add)
+    ms(t_("ones"), 1.0)
+    ms(t_("RB"), 0.0)
+    ts(t_("RB", 112, 128), t_("ir", 0, 16), PM, None, OP.is_equal)
+    for c in range(STEPS):
+        ms(t_("CZ", 4096, 4112, c), 0.0)
+    for s in range(8):
+        ms(t_("SC", s, 128, step=8), float(1 << (7 - s)))
+    tt(t_("Gs"), t_("Gf"), t_("SC"), OP.mult)
+    ts(t_("wSh"), t_("Gs"), WH, None, OP.mult)
+    ts(t_("wSl"), t_("Gs"), WL, None, OP.mult)
+    ts(t_("ln32"), t_("ln32"), PM, None, OP.add)
+    ts(t_("ba32"), t_("ln32"), 16.0, 256.0, OP.mult, OP.add)
+    ts(t_("tp32"), t_("ln32"), 16.0, None, OP.add)
+    tt(t_("tp32"), t_("tp32"), t_("ls32"), OP.mult)
+    ts(t_("sp32"), t_("ln32"), -15.0, 3856.0, OP.mult, OP.add)
+    tt(t_("sp32"), t_("sp32"), t_("tp32"), OP.subtract)
+    for k in range(3):
+        ts(t_("C48", 16 * k, 16 * k + 16), t_("lnO"), 256.0 * k, None, OP.add)
+
+    def zt(t, a=0, b=256, step=1):
+        return t_("CZ", 4112 + a, 4112 + b, t, step)
+
+    def early(t):
+        z = zt(t)
+        for r in range(16):
+            for k, w in enumerate(("wEh", "wEl")):
+                mm(p_(2, 320, 336), t_(w, 15 - r, 143 - r), zt(t, r, 256, 16), r == 0 and k == 0, r == 15 and k == 1)
+        cp(t_("ui", c=t), p_(2, 320, 336))
+        ts(t_("u", c=t), t_("ui", c=t), 4095, None, OP.bitwise_and)
+        tt(t_("sq", c=t), t_("u", c=t), t_("u", c=t), OP.mult)
+        ts(t_("u37", c=t), t_("u", c=t), 37.0, None, OP.mult)
+        ts(t_("sh", c=t), t_("sq", c=t), 5, None, OP.arith_shift_right)
+        tt(t_("base", c=t), t_("sh", c=t), t_("u37", c=t), OP.add)
+        ts(t_("vb", c=t), t_("base", c=t), 1023, None, OP.bitwise_and)
+        ts(t_("b2", c=t), t_("vb", c=t), -512.0, None, OP.mult)
+        tt(t_("b1", c=t), t_("b2", c=t), t_("lnH"), OP.subtract)
+        tt(t_("Zf", c=t), ind(t_("b1", c=t), t_("bc")), t_("mO"), OP.mult)
+        mm(p_(3, 256, 512), t_("Gf"), t_("Zf", c=t), True, True, f32=True)
+        for j in range(16):
+            n = 16 * (j + 1)
+            act(t_("junk", 0, n, 2 * j), p_(3, 256, 256 + n), AF.Sign, bias=t_("b1", j, j + 1, t), scale=-1.0, acc=t_("c1", j, j + 1, t))
+            act(t_("junk", 0, n, 2 * j + 1), p_(3, 256, 256 + n), AF.Sign, bias=t_("b2", j, j + 1, t), scale=-1.0, acc=t_("c2", j, j + 1, t))
+        tt(t_("dd", c=t), t_("c2", c=t), t_("c1", c=t), OP.subtract)
+        ts(t_("dup", c=t), t_("dd", c=t), 2.0, None, OP.is_ge)
+
+    def step(t):
+        if t == 0:
+            early(0)
+        z = zt(t)
+        mm(p_(0, 0, 256), t_("I"), z, True, True)
+        iota(flt(t_("NEW", c=t)), [[16, 256]], t)
+        if t:
+            ts(t_("vA", c=t), t_("base", c=t), t_("A", 0, 1, t - 1), None, OP.add)
+            ts(t_("v", c=t), t_("vA", c=t), 1023, None, OP.bitwise_and)
+        else:
+            ts(t_("v", c=t), t_("base", c=t), 1023, None, OP.bitwise_and)
+        cp(t_("vl", c=t), t_("v", c=t))
+        vl, wl = t_("vl", c=t), t_("wl", c=t)
+        cp(t_("boff", c=t), ind(t_("btab" if t else "bki", 0, 1024), vl))
+        tt(t_("dv", c=t), t_("lnD"), t_("v", c=t), OP.subtract)
+        tt(t_("dw", c=t), t_("dv", c=t), t_("dup", c=t), OP.mult)
+        tt(t_("wo", c=t), t_("v", c=t), t_("dw", c=t), OP.add)
+        cp(wl, t_("wo", c=t))
+        for c in range(4):
+            act(t_("CZ", 1024 * c, 1024 * c + 1024, t), ind(t_("geno_s"), t_("boff", 64 * c, 64 * c + 64, t)), AF.Copy)
+        keep(t_("geno_s", t, 4096, step=16), z)
+        if t == STEPS - 1:
+            store("sg", T.ygeno[:], t_("geno_s"))
+        tt(t_("db", c=t), ind(t_("btab", 0, 1024), vl), t_("NEW", c=t), OP.subtract)
+        act(t_("qg", c=t), ind(t_("qtab", 0, 1024), vl), AF.Copy)
+        act(t_("ig", c=t), ind(t_("itab", 0, 1024), vl), AF.Copy)
+        act(t_("im1", c=t), t_("ig", c=t), AF.Identity, bias=-1.0)
+        ts(t_("fl", c=t), t_("qg", c=t), float(t + 1), None, OP.is_ge)
+        tt(t_("gt", c=t), t_("ig", c=t), p_(0, 0, 256), OP.is_lt)
+        gk = ("key", t)
+        mm(p_(1, 0, 256), t_("I"), t_("C16"), True, False, gk, "first")
+        mm(p_(2, 0, 256), t_("I"), t_("C16"), True, False)
+        for h in range(2):
+            mm(p_(2, 128 * h, 128 * h + 128), t_("qg", 128 * h, 128 * h + 128, t), t_("I16"), False, h == 1)
+        for h in range(2):
+            mm(p_(2, 256 + 8 * h, 264 + 8 * h), t_("fl", 128 * h, 128 * h + 128, t), t_("Gm", 0, 8), True, True)
+        for h in range(4):
+            mm(p_(2, 272 + 8 * h, 280 + 8 * h), t_("gt", 128 * (h % 2), 128 * (h % 2) + 128, t), t_("Gm", 0, 8), True, True)
+        act(t_("qks", c=t), p_(2, 1, 256, 2), AF.Copy)
+        ts(t_("n1", c=t), p_(2, 272, 304), 9.0, 4194304.0, OP.is_lt, OP.mult)
+        ts(t_("nsB", c=t), t_("n1", c=t), BIG, None, OP.max)
+        if t + 1 < STEPS:
+            ts(t_("sk", c=t), p_(2, 272, 288), 9.0, 2.0, OP.is_ge, OP.mult)
+            tt(t_("ac", c=t), t_("sk", c=t), p_(2, 256, 272), OP.min)
+            mm(p_(2, 304, 320), t_("ones"), t_("ac", c=t), True, True)
+            red(t_("A", 0, 1, t), p_(2, 304, 320))
+        tt(t_("q1", c=t), p_(2, 0, 256, 2), t_("qks", c=t), OP.max)
+        tt(t_("q2", c=t), t_("q1", 0, 128, t, 2), t_("q1", 1, 128, t, 2), OP.max)
+        tt(t_("q3", c=t), t_("q2", 0, 64, t, 2), t_("q2", 1, 64, t, 2), OP.max)
+        tt(t_("m0", c=t), t_("q3", 0, 32, t, 2), t_("q3", 1, 32, t, 2), OP.max)
+        if t + 1 < STEPS:
+            early(t + 1)
+        for h in range(2):
+            mm(p_(1, 128 * h, 128 * h + 128), t_("fl", 128 * h, 128 * h + 128, t), t_("IB"), False, False, gk, "mid")
+            for k in range(16):
+                mm(p_(1, 128 * h + k, 128 * h + 128, 16), t_("CZ", 2048 * h + k, 2048 * h + 2048, t, 16), t_("G32", 0, 8), False, False, gk, "mid")
+            for k in range(16):
+                if h == 0:
+                    tt(t_("mx", 128 * k, 128 * k + 128, t), t_("CZ", k, 2048, t, 16), p_(0, 0, 128), OP.max)
+                else:
+                    for e in range(2):
+                        o = 2048 + 128 * k + 64 * e
+                        tt(t_("mx", o, o + 64, t), t_("CZ", 2048 + 1024 * e + k, 3072 + 1024 * e, t, 16), p_(0, 128 + 64 * e, 192 + 64 * e), OP.max)
+            for k in range(16):
+                o = 2048 * h + 128 * k
+                end = h == 1 and k == 15
+                mm(p_(1, 128 * h + k, 128 * h + 128, 16), t_("mx", o, o + 128, t), t_("G64", 0, 8), False, end, gk, "last" if end else "mid")
+        act(t_("keys", c=t), p_(1, 0, 256), AF.Copy)
+        ko = t_("keys", 1, 256, t, 2)
+        tt(t_("h1"), p_(1, 0, 256, 2), ko, OP.max)
+        tt(t_("l1"), p_(1, 0, 256, 2), ko, OP.min)
+        for a, b, n in (("1", "2", 128), ("2", "3", 64), ("3", "4", 32)):
+            he, ho, le, lo = t_("h" + a, 0, n, step=2), t_("h" + a, 1, n, step=2), t_("l" + a, 0, n, step=2), t_("l" + a, 1, n, step=2)
+            tt(t_("HL", 0, 16, t) if b == "4" else t_("h" + b), he, ho, OP.max)
+            tt(t_("mn" + b), he, ho, OP.min)
+            tt(t_("ml" + b), le, lo, OP.max)
+            tt(t_("HL", 16, 32, t) if b == "4" else t_("l" + b), t_("mn" + b), t_("ml" + b), OP.max)
+        HL = t_("HL", c=t)
+        cp(t_("HI", c=t), HL)
+        tt(t_("flg", c=t), HL, t_("nsB", c=t), OP.is_ge)
+        ts(t_("HA", c=t), t_("HI", c=t), 511, None, OP.bitwise_and)
+        tt(t_("thr", c=t), t_("HL", 16, 32, t), t_("nsB", 0, 16, t), OP.max)
+        tt(t_("KM", c=t), t_("HA", c=t), t_("flg", c=t), OP.mult)
+        tt(t_("kx", c=t), t_("KM", 0, 16, t), t_("KM", 16, 32, t), OP.max)
+        tt(t_("sm", c=t), t_("kx", c=t), t_("m0", c=t), OP.max)
+        ts(t_("si", c=t), t_("sm", c=t), -1.0, 256.0, OP.mult, OP.add)
+        ts(t_("sl", c=t), t_("si", c=t), 15, None, OP.bitwise_and)
+        tt(t_("awsl", 256, 512, t), ind(t_("sl", c=t), t_("bc")), t_("kidx"), OP.not_equal)
+        tt(t_("awsl", 0, 256, t), ind(t_("thr", c=t), t_("bc")), t_("keys", c=t), OP.is_gt)
+        for x in (2, 3, 0, 1):
+            mm(p_(4, 128 * x, 128 * x + 128), t_("awsl", 128 * x, 128 * x + 128, t), t_("I"), True, True)
+        tt(t_("tb"), p_(4, 256, 512), t_("db", c=t), OP.mult)
+        tt(ind(t_("btab"), wl), t_("tb"), t_("NEW", c=t), OP.add)
+        tt(t_("t1"), p_(4, 0, 256), t_("qg", c=t), OP.mult)
+        act(t_("t2"), t_("t1"), AF.Identity, bias=-float(8 + t))
+        tt(t_("t3"), p_(4, 256, 512), t_("t2"), OP.mult)
+        ts(ind(t_("qtab"), wl), t_("t3"), 1.0, float(8 + t), OP.mult, OP.add)
+        for j in range(8):
+            act(t_("Y", 32 * j, 32 * j + 32, t), t_("KM", c=t), AF.Copy, scale=t_("Gmf", j, j + 1))
+        for k in range(8):
+            mm(p_(5, 0, 32), t_("RB", 112 - 16 * k, 240 - 16 * k), t_("Y", k, 256, t, 8), k == 0, k == 7)
+        ts(t_("mz"), p_(5, 0, 32), 0.0, None, OP.is_equal)
+        tt(t_("bm"), t_("ba32"), p_(5, 0, 32), OP.subtract)
+        tt(t_("tm"), t_("mz"), t_("sp32"), OP.mult)
+        tt(t_("of"), t_("tm"), t_("bm"), OP.add)
+        for x in range(4):
+            cp(t_("al", 8 * x, 8 * x + 8, t), t_("of", x, 32, 0, 4))
+        act(t_("CZ", 4368, 4880, t), ind(t_("CZ", 0, 4368, t), t_("al", c=t)), AF.Copy)
+        a12, a1, a2 = t_("CZ", 4368, 4880, t), t_("CZ", 4368, 4624, t), t_("CZ", 4624, 4880, t)
+        mm(p_(6, 0, 512), t_("nI"), a12, True, False)
+        mm(p_(6, 0, 256), t_("I"), z, False, False)
+        mm(p_(6, 256, 512), t_("I"), z, False, True)
+        mm(p_(7, 0, 256), t_("I"), a1, True, False)
+        mm(p_(7, 0, 256), t_("nI"), a2, False, True)
+        act(t_("SG", 0, 512), p_(6, 0, 512), AF.Sign, bias=-0.5, scale=-1.0)
+        act(t_("SG", 512, 1024), p_(6, 0, 512), AF.Sign, bias=-0.5)
+        act(t_("SG", 1024, 1280), p_(7, 0, 256), AF.Sign, bias=-0.5, scale=-1.0)
+        act(t_("SG", 1280, 1536), p_(7, 0, 256), AF.Sign, bias=-0.5)
+        for r in range(16):
+            mm(p_(5, 64, 160), t_("EB", 15 - r, 143 - r), t_("SG", r, 1536, 0, 16), r == 0, r == 15)
+        ts(t_("TH"), p_(5, 64, 160), 2.0, 1024.0, OP.is_ge, OP.mult)
+        tt(t_("KK", 0, 16), t_("TH", 0, 16), t_("TH", 16, 32), OP.add)
+        tt(t_("KK", 16, 48), t_("TH", 32, 64), t_("TH", 64, 96), OP.add)
+        tt(t_("KL"), t_("KK"), t_("C48"), OP.add)
+        k0, k1, k2 = t_("KL", 0, 16), t_("KL", 16, 32), t_("KL", 32, 48)
+        tt(t_("mna"), k0, k1, OP.min)
+        tt(t_("mxa"), k0, k1, OP.max)
+        tt(t_("FM", 0, 16), t_("mna"), k2, OP.min)
+        tt(t_("tta"), t_("mxa"), k2, OP.min)
+        tt(t_("FM", 16, 32), t_("mna"), t_("tta"), OP.max)
+        cp(t_("FI"), t_("FM"))
+        ts(t_("FA"), t_("FI"), 1023, None, OP.bitwise_and)
+        cp(t_("fml", c=t), t_("FA"))
+        win = t_("CZ", 4112, 4880, t)
+        if t + 2 < STEPS:
+            f, m = t_("fmb", 0, 256), t_("fmb", 256, 512)
+            act(t_("fmb"), ind(win, t_("fml", c=t)), AF.Copy)
+            act(t_("ff"), f, AF.Copy)
+            mm(p_(6, 0, 256), t_("I"), f, True, False)
+            mm(p_(6, 0, 256), t_("nI"), m, False, True)
+            mm(p_(7, 256, 512), t_("wSh"), z, True, False)
+            mm(p_(7, 256, 512), t_("wSl"), z, False, True)
+            cp(t_("bti", c=t), p_(7, 256, 512))
+            ts(t_("bit", c=t), t_("bti", c=t), 128, None, OP.bitwise_and)
+            tt(t_("tX"), p_(6, 0, 256), t_("bit", c=t), OP.mult)
+            mm(p_(6, 256, 512), t_("I"), m, True, False)
+            mm(p_(6, 256, 512), t_("Is"), t_("tX"), False, True)
+            act(t_("cb", c=t), p_(6, 256, 512), AF.Copy)
+            send(t_("cb", c=t), t + 2, (rank + 2) % n_ranks)
+        else:
+            act(t_("ff"), ind(win, t_("fml", 0, 16, t)), AF.Copy)
+        tt(ind(t_("itab"), wl), t_("im1", c=t), t_("ff"), OP.max)
+
+    for t in range(STEPS):
+        step(t)
+    act(t_("yi", 0, 512), t_("itab", 0, 512), AF.Copy)
+    cp(t_("yi", 512, 1024), t_("itab", 512, 1024))
+    for k in range(2):
+        store("si%d" % k, T.yimm[:, 512 * k:512 * k + 512], t_("yi", 512 * k, 512 * k + 512))
+    for k, b in ((0, 4), (1, 1)):
+        act(p_(b, 0, 512), t_("qtab", 512 * k, 512 * k + 512), AF.Copy, scale=4096.0)
+        tt(t_("yb", 512 * k, 512 * k + 512), t_("btab", 512 * k, 512 * k + 512), p_(b, 0, 512), OP.add)
+        store("sb%d" % k, T.ybank[:, 512 * k:512 * k + 512], t_("yb", 512 * k, 512 * k + 512))
+
+    n = len(ops)
+    for i in range(n):
+        if "proxy" in ops[i]:
+            edges[i][ops[i]["proxy"]] = 0
+    succ = [[] for _ in range(n)]
+    for i in range(n):
+        for j, w in edges[i].items():
+            l = lag.get(j, ops[j]["cost"]) + (COST["wake"] if w else 0.0)
+            if "proxy" in ops[i]:
+                l = COST["link"]
+            succ[j].append((i, l))
+    prio = [0.0] * n
+    for j in range(n - 1, -1, -1):
+        prio[j] = max([lag.get(j, ops[j]["cost"])] + [l + prio[i] for i, l in succ[j]])
+    order = list_schedule(n, [o["q"] for o in ops], [o["cost"] for o in ops], succ, [len(e) for e in edges],
+                          [prio[i] + BIAS.get(ops[i]["tag"], 0.0) for i in range(n)])[0]
+
+    eng = {"v": g.vector, "s": g.scalar, "p": g.tensor, "g": g, "y": g.sync}
+    total = {}
+    at = [None] * n
+    know = {q: {} for q in eng}
+    snap = [None] * n
+    for i in order:
+        o = ops[i]
+        q = o["q"]
+        if q == "n":
+            at[i] = (o["sem"], o["inc"])
+            snap[i] = {o["sem"]: o["inc"]}
+            total[o["sem"]] = o["inc"]
+            continue
+        k = know[q]
+        want = {}
+        for j, w in edges[i].items():
+            if w and at[j] is not None:
+                s, v = at[j]
+                if k.get(s, 0) < v and want.get(s, (0, 0))[0] < v:
+                    want[s] = (v, j)
+        for s in list(want):
+            v, j = want[s]
+            if any(s2 != s and snap[j2].get(s, 0) >= v for s2, (v2, j2) in want.items()):
+                del want[s]
+        for s, (v, j) in want.items():
+            eng[q].wait_ge(T.sem[s], v)
+            for s2, v2 in snap[j].items():
+                if k.get(s2, 0) < v2:
+                    k[s2] = v2
+        ins = o["emit"]()
+        if o["sem"] is not None:
+            total[o["sem"]] = total.get(o["sem"], 0) + o["inc"]
+            ins.then_inc(T.sem[o["sem"]], o["inc"])
+            at[i] = (o["sem"], total[o["sem"]])
+            snap[i] = dict(k)
+            snap[i][o["sem"]] = total[o["sem"]]
+        if "remote" in o:
+            total["rl"] = total.get("rl", 0) + o["remote"]
+    for s in sorted(total):
+        if know["g"].get(s, 0) < total[s]:
+            g.wait_ge(T.sem[s], total[s])

@@ -8,45 +8,45 @@ TILES = {
     "bt": (256, "bfloat16", 1), "geno_s": (4096, "bfloat16", 1), "bk": (1024, "int32", 1), "im0": (1024, "bfloat16", 1),
     "wti": (1, "int32", 1), "btab": (1280, "float32", 1), "qtab": (1280, "float32", 1), "itab": (1280, "float32", 1),
     "cb": (256, "bfloat16", 4),
-    "CZ": (4880, "bfloat16", 6), "mx": (4096, "bfloat16", 2),
+    "CZ": (6416, "bfloat16", 6), "mx": (4096, "bfloat16", 2),
     "bki": (1024, "int32", 1), "qki": (1024, "int32", 1),
     "yb": (1024, "float32", 1), "yi": (1024, "bfloat16", 1),
     "pI": (8, "int32", 1), "pM": (8, "int32", 1), "pG": (8, "int32", 1), "pf": (32, "float32", 1), "wf": (16, "float32", 1), "wi2": (16, "int32", 1),
     "ic": (256, "float32", 1), "icg": (128, "float32", 1), "ir": (256, "float32", 1),
     "I": (128, "bfloat16", 1), "nI": (128, "bfloat16", 1), "IB": (128, "bfloat16", 1), "I16": (128, "bfloat16", 1), "Is": (128, "bfloat16", 1),
-    "Gf": (128, "float32", 1), "Gs": (128, "float32", 1), "SC": (128, "float32", 1), "wSh": (128, "bfloat16", 1), "wSl": (128, "bfloat16", 1),
+    "row16": (256, "bfloat16", 1), "nD": (128, "bfloat16", 2), "nIt": (128, "bfloat16", 6), "lc": (16, "float32", 1),
+    "Gf": (128, "bfloat16", 1), "Gs": (128, "float32", 1), "SC": (128, "float32", 1), "wSh": (128, "bfloat16", 1), "wSl": (128, "bfloat16", 1),
     "Gm": (16, "bfloat16", 1), "Gmf": (8, "float32", 1), "G64": (16, "bfloat16", 1), "G32": (16, "bfloat16", 1),
-    "EB": (144, "bfloat16", 1), "wEh": (144, "bfloat16", 1), "wEl": (144, "bfloat16", 1), "RB": (240, "bfloat16", 1),
-    "mO": (256, "float32", 1), "C16": (256, "bfloat16", 1), "ones": (128, "bfloat16", 1), "kidx": (256, "int32", 1),
-    "bci": (16, "int32", 1), "bc": (16, "uint16", 1), "lnO": (16, "float32", 1), "lnD": (16, "float32", 1), "lnH": (16, "float32", 1), "C48": (48, "float32", 1),
+    "EB": (144, "bfloat16", 1), "wE": (144, "float16", 1), "ww": (32, "float32", 1), "RB": (240, "bfloat16", 1),
+    "C16": (256, "bfloat16", 1), "ones": (128, "bfloat16", 1), "kidx": (256, "int32", 1),
+    "bci": (16, "int32", 1), "bc": (16, "uint16", 1), "lnO": (16, "float32", 1), "lnD": (16, "float32", 1), "LR": (2048, "float16", 1), "Mk": (256, "bfloat16", 1), "m1": (256, "bfloat16", 1), "C48": (48, "float32", 1),
     "ln32": (32, "float32", 1), "ls32": (32, "float32", 1), "tp32": (32, "float32", 1), "ba32": (32, "float32", 1), "sp32": (32, "float32", 1),
-    "NEW": (256, "float32", 2),
     "ui": (16, "int32", 2), "u": (16, "int32", 2), "sq": (16, "int32", 2), "sh": (16, "int32", 2), "u37": (16, "int32", 2), "base": (16, "int32", 2),
-    "vb": (16, "int32", 2), "dd": (16, "float32", 2), "b1": (16, "float32", 2), "b2": (16, "float32", 2),
-    "Zf": (256, "float32", 2), "junk": (256, "bfloat16", 8), "c1": (16, "float32", 2), "c2": (16, "float32", 2),
+    "vb": (16, "int32", 2), "vh": (16, "float16", 2), "bb": (16, "float32", 2), "cs": (16, "float32", 2), "ri": (16, "int32", 2), "fr": (16, "float32", 2),
+    "junk": (256, "bfloat16", 8), "c1": (16, "float32", 2), "c2": (16, "float32", 2),
     "bti": (256, "int32", 2), "bit": (256, "int32", 2),
     "vA": (16, "int32", 2), "v": (16, "int32", 2), "vl": (16, "uint16", 2), "dup": (16, "float32", 2), "dv": (16, "float32", 2), "dw": (16, "float32", 2),
     "wo": (16, "float32", 2), "wl": (16, "uint16", 2),
-    "boff": (256, "uint16", 2), "db": (256, "float32", 2), "qg": (256, "bfloat16", 2), "ig": (256, "bfloat16", 2), "im1": (256, "float32", 2),
+    "boff": (256, "uint16", 2), "bg": (256, "float32", 2), "ns": (256, "float32", 1), "qg": (256, "bfloat16", 2), "im1": (256, "float32", 2),
     "fl": (256, "bfloat16", 2), "gt": (256, "bfloat16", 2), "qks": (128, "float32", 2), "q1": (128, "float32", 2), "q2": (64, "float32", 2), "q3": (32, "float32", 2),
     "m0": (16, "float32", 2), "n1": (32, "float32", 2), "nsB": (32, "float32", 2), "sk": (16, "float32", 2), "ac": (16, "bfloat16", 2), "A": (8, "float32", 2),
     "keys": (256, "float32", 2), "h1": (128, "float32", 1), "l1": (128, "float32", 1), "h2": (64, "float32", 1), "mn2": (64, "float32", 1), "ml2": (64, "float32", 1), "l2": (64, "float32", 1),
     "h3": (32, "float32", 1), "mn3": (32, "float32", 1), "ml3": (32, "float32", 1), "l3": (32, "float32", 1), "mn4": (16, "float32", 1), "ml4": (16, "float32", 1),
     "HL": (32, "float32", 2), "flg": (32, "float32", 2), "HI": (32, "int32", 2), "HA": (32, "int32", 2), "KM": (32, "float32", 2), "thr": (16, "float32", 2),
     "kx": (16, "float32", 2), "sm": (16, "float32", 2), "si": (16, "int32", 2), "sl": (16, "int32", 2), "awsl": (512, "bfloat16", 2),
-    "tb": (256, "float32", 1), "t1": (256, "bfloat16", 1), "t2": (256, "bfloat16", 1), "t3": (256, "float32", 1),
+    "tb": (256, "float32", 1), "t1": (256, "float32", 1), "t2": (256, "float32", 1),
     "Y": (256, "bfloat16", 2), "mz": (32, "float32", 1), "tm": (32, "float32", 1), "bm": (32, "float32", 1), "of": (32, "float32", 1), "al": (32, "uint16", 2),
     "SG": (1536, "bfloat16", 1), "TH": (96, "float32", 1), "KK": (48, "float32", 1), "KL": (48, "float32", 1), "mna": (16, "float32", 1), "mxa": (16, "float32", 1), "tta": (16, "float32", 1),
     "FM": (32, "float32", 1), "FI": (32, "int32", 1), "FA": (32, "int32", 1), "fml": (32, "uint16", 2), "fmb": (512, "bfloat16", 1), "ff": (256, "float32", 1), "tX": (256, "bfloat16", 1),
 }
-BYTES = {"float32": 4, "int32": 4, "bfloat16": 2, "uint16": 2}
+BYTES = {"float32": 4, "int32": 4, "bfloat16": 2, "uint16": 2, "float16": 2}
 PLACE = {}
 _size = {d: 0 for d in BYTES}
 for _n, (_w, _d, _c) in TILES.items():
     _p = (_w + 15) // 16 * 16
     PLACE[_n] = (_size[_d], _p)
     _size[_d] += _p * _c
-BUF = {"float32": "bigf", "int32": "bigi", "bfloat16": "bigb", "uint16": "bigu"}
+BUF = {"float32": "bigf", "int32": "bigi", "bfloat16": "bigb", "uint16": "bigu", "float16": "bigh"}
 SCRATCH = {BUF[_d]: ("sbuf", [128, _size[_d]], _d) for _d in BYTES}
 for _k in range(8):
     SCRATCH["P%d" % _k] = ("psum", [128, 512], "float32")
@@ -55,9 +55,14 @@ STORES = ["sg", "sb0", "sb1", "si0", "si1"]
 SEMAPHORES = ["qv", "qs", "qp", "qg", "rl"] + ["arr%d" % t for t in range(1, STEPS)] + ["ld_" + n for n in LOADS] + ["st_" + n for n in STORES]
 
 
-BIAS = {'ic': -8, 'qtab': -7, 'qki': -8, 'P4awsl': -1, 'v': 16, 'ln32': 2, 'bci': 9, 'thr': -13, 'I': 18, 'P6nI': -10, 'SC': 5, 'KL': 19, 'mO': -21, 'ir': 4, 'ba32': -5, 'tb': -2, 'RB': -1, 'ls32': 14, 'HL': -21, 'mn4': -3, 'P2wEh': 3, 'ac': 7, 'geno_s': -18, 'ml3': -2, 'db': -3, 'Gm': -2, 'P1CZ': 9, 'NEW': 2, 'sm': -1, 'lnH': -1, 'outsi1': 9, 'wti': -13, 'P1fl': 3, 'P4qtab': -1, 'vA': 8}
+BIAS = {'C48': -8, 'CZ': 2, 'G64': 14, 'Gm': 9, 'Gs': 10, 'I': 20, 'KK': -9, 'LR': -1, 'P1fl': 3, 'P2fl': 8, 'P2ones': -14, 'P3I': -1, 'P4awsl': -1,
+        'P4qtab': 3, 'P6I': 2, 'P6nI': -7, 'SC': 6, 'ac': 12, 'al': -3, 'ba32': -6, 'base': 3, 'bb': 5, 'bci': 17, 'bk': -13, 'btab': 3, 'bti': -4,
+        'c1': 4, 'cs': -12, 'flg': 13, 'geno_s': -27, 'ic': -10, 'im0': 3, 'ir': -2, 'itab': -1, 'keys': 11, 'kidx': -3, 'lnD': -6, 'lnO': 2,
+        'ls32': 7, 'm0': -1, 'm1': 3, 'ml4': -4, 'mn4': -6, 'n1': 11, 'nI': -11, 'ns': 1, 'of': -4, 'outsb1': 1, 'outsi1': 6, 'pG': 3, 'qki': -8,
+        'qtab': -5, 'sh': 1, 'sk': 3, 'sm': -1, 'sp32': 9, 't1': 8, 'thr': -6, 'tp32': -1, 'v': 31, 'vh': 4, 'vl': 19, 'wi2': 1, 'wo': -4, 'wti': -7}
 COST = {"us": 0.00083 * 1.25, "ps": 0.00071 * 1.25, "gather": 1.56, "scatter": 3.8, "wake": 0.08, "link": 4.0}
 LOOK = 0.3
+VG = {t: 512 for t in range(STEPS)}
 
 
 def list_schedule(n, que, cost, succ, need, prio):
@@ -105,6 +110,42 @@ def list_schedule(n, que, cost, succ, need, prio):
                 ready.setdefault(que[i], []).append(i)
                 dirty.add(que[i])
     return order, end
+
+
+def best_order(n, que, cost, succ, prio, rounds=2):
+    need = [0] * n
+    for j in range(n):
+        for i, l in succ[j]:
+            need[i] += 1
+    back = [[] for _ in range(n)]
+    for j in range(n):
+        for i, l in succ[j]:
+            back[i].append((j, max(0.0, cost[i] + l - cost[j])))
+    bneed = [len(x) for x in succ]
+
+    def starts(order, follow):
+        at, when, free = [0.0] * n, [0.0] * n, {}
+        for i in order:
+            st = when[i]
+            if que[i] != "n":
+                st = max(st, free.get(que[i], 0.0))
+                free[que[i]] = st + cost[i]
+            at[i] = st
+            for k, l in follow[i]:
+                if st + l > when[k]:
+                    when[k] = st + l
+        return at
+    best = None
+    for k in range(rounds):
+        order, end = list_schedule(n, que, cost, succ, need, prio)
+        if best is None or end < best[1]:
+            best = (order, end)
+        if k + 1 < rounds:
+            at = starts(order, succ)
+            rev = list_schedule(n, que, cost, back, bneed, [at[i] + cost[i] for i in range(n)])[0]
+            at = starts(rev, back)
+            prio = [at[i] + cost[i] for i in range(n)]
+    return best
 
 
 def rank_program(g, core, T, topo):
@@ -305,13 +346,14 @@ def rank_program(g, core, T, topo):
     WH, WL = t_("wf", 0, 1), t_("wf", 8, 9)
     cp(WH, t_("wi2", 0, 1))
     cp(WL, t_("wi2", 8, 9))
-    ts(t_("wEh"), t_("EB"), WH, None, OP.mult)
-    ts(t_("wEl"), t_("EB"), WL, None, OP.mult)
+    WF, WG, WS = t_("ww", 0, 1), t_("ww", 8, 9), t_("ww", 16, 17)
+    cp(WF, t_("wti"))
+    ts(WG, WF, 2047.5, -4096.0, OP.is_gt, OP.mult)
+    tt(WS, WF, WG, OP.add)
+    ts(t_("wE"), t_("EB"), WS, None, OP.mult)
     ts(t_("lnO"), t_("lnO"), PM, None, OP.add)
     ts(t_("lnD"), t_("lnO"), 1024.0, None, OP.add)
-    ts(t_("lnH"), t_("lnO"), 0.5, None, OP.add)
     cp(t_("bc"), t_("bci"))
-    ts(t_("mO"), t_("ir"), PM, None, OP.is_equal)
     ts(t_("Gf"), t_("icg"), PG, None, OP.is_equal)
     ts(t_("I"), t_("ic", 0, 128), P, None, OP.is_equal)
     ts(t_("bki"), t_("bk"), 4095, None, OP.bitwise_and)
@@ -330,6 +372,18 @@ def rank_program(g, core, T, topo):
     ms(t_("ones"), 1.0)
     ms(t_("RB"), 0.0)
     ts(t_("RB", 112, 128), t_("ir", 0, 16), PM, None, OP.is_equal)
+    for r in range(16):
+        ts(t_("LR", 128 * r, 128 * r + 128), t_("Gf"), t_("RB", 112 + r, 113 + r), None, OP.mult)
+    iota(flt(t_("row16")), [[16, 256]])
+    for h in range(2):
+        ts(t_("lc", 8 * h, 8 * h + 1), P, -16.0, -2048.0 * h, OP.mult, OP.add)
+        ts(t_("nD", c=h), t_("I"), t_("lc", 8 * h, 8 * h + 1), None, OP.mult)
+    for t in range(1, STEPS):
+        ts(t_("nIt", c=t), t_("I"), float(-t), None, OP.mult)
+    ts(t_("Mk"), t_("ir"), PM, 2048.0, OP.is_ge, OP.mult)
+    for c in range(2):
+        ms(t_("c1", 0, 1, c), 0.0)
+    ms(t_("m1"), -1.0)
     for c in range(STEPS):
         ms(t_("CZ", 4096, 4112, c), 0.0)
     for s in range(8):
@@ -352,8 +406,7 @@ def rank_program(g, core, T, topo):
     def early(t):
         z = zt(t)
         for r in range(16):
-            for k, w in enumerate(("wEh", "wEl")):
-                mm(p_(2, 320, 336), t_(w, 15 - r, 143 - r), zt(t, r, 256, 16), r == 0 and k == 0, r == 15 and k == 1)
+            mm(p_(2, 320, 336), t_("wE", 15 - r, 143 - r), zt(t, r, 256, 16), r == 0, r == 15)
         cp(t_("ui", c=t), p_(2, 320, 336))
         ts(t_("u", c=t), t_("ui", c=t), 4095, None, OP.bitwise_and)
         tt(t_("sq", c=t), t_("u", c=t), t_("u", c=t), OP.mult)
@@ -361,23 +414,29 @@ def rank_program(g, core, T, topo):
         ts(t_("sh", c=t), t_("sq", c=t), 5, None, OP.arith_shift_right)
         tt(t_("base", c=t), t_("sh", c=t), t_("u37", c=t), OP.add)
         ts(t_("vb", c=t), t_("base", c=t), 1023, None, OP.bitwise_and)
-        ts(t_("b2", c=t), t_("vb", c=t), -512.0, None, OP.mult)
-        tt(t_("b1", c=t), t_("b2", c=t), t_("lnH"), OP.subtract)
-        tt(t_("Zf", c=t), ind(t_("b1", c=t), t_("bc")), t_("mO"), OP.mult)
-        mm(p_(3, 256, 512), t_("Gf"), t_("Zf", c=t), True, True, f32=True)
-        for j in range(16):
-            n = 16 * (j + 1)
-            act(t_("junk", 0, n, 2 * j), p_(3, 256, 256 + n), AF.Sign, bias=t_("b1", j, j + 1, t), scale=-1.0, acc=t_("c1", j, j + 1, t))
-            act(t_("junk", 0, n, 2 * j + 1), p_(3, 256, 256 + n), AF.Sign, bias=t_("b2", j, j + 1, t), scale=-1.0, acc=t_("c2", j, j + 1, t))
-        tt(t_("dd", c=t), t_("c2", c=t), t_("c1", c=t), OP.subtract)
-        ts(t_("dup", c=t), t_("dd", c=t), 2.0, None, OP.is_ge)
+        cp(t_("vh", c=t), t_("vb", c=t))
+        for b in (256, 0):
+            if b == 0:
+                mm(p_(3, 0, 256), t_("I"), t_("Mk"), True, False)
+            for r in range(16):
+                mm(p_(3, b + r, b + 256, 16), t_("LR", 128 * r, 128 * r + 128), t_("vh", c=t), b == 256, b == 256 or r == 15)
+        ts(t_("bb", c=t), t_("vb", c=t), -32.0, -5.7, OP.mult, OP.add)
+        for j in range(15, -1, -1):
+            if j:
+                act(t_("junk", 0, 16 * j, 2 * j), p_(3, 256, 256 + 16 * j), AF.Sigmoid, bias=t_("bb", j, j + 1, t), scale=32.0, acc=t_("c1", j, j + 1, t))
+            act(t_("junk", 0, 16, 2 * j + 1), p_(3, 16 * j, 16 * j + 16), AF.Sigmoid, bias=t_("bb", j, j + 1, t), scale=32.0, acc=t_("c2", j, j + 1, t))
+        tt(t_("cs", c=t), t_("c1", c=t), t_("c2", c=t), OP.add)
+        ts(t_("ri", c=t), t_("cs", c=t), -0.45, None, OP.add)
+        tt(t_("fr", c=t), t_("cs", c=t), t_("ri", c=t), OP.subtract)
+        ts(t_("dup", c=t), t_("fr", c=t), 0.0017, None, OP.is_gt)
 
     def step(t):
         if t == 0:
             early(0)
         z = zt(t)
         mm(p_(0, 0, 256), t_("I"), z, True, True)
-        iota(flt(t_("NEW", c=t)), [[16, 256]], t)
+        mm(p_(0, 256, 512), t_("I"), z, True, False)
+        mm(p_(0, 256, 512), t_("I"), t_("m1"), False, True)
         if t:
             ts(t_("vA", c=t), t_("base", c=t), t_("A", 0, 1, t - 1), None, OP.add)
             ts(t_("v", c=t), t_("vA", c=t), 1023, None, OP.bitwise_and)
@@ -391,16 +450,18 @@ def rank_program(g, core, T, topo):
         tt(t_("wo", c=t), t_("v", c=t), t_("dw", c=t), OP.add)
         cp(wl, t_("wo", c=t))
         for c in range(4):
-            act(t_("CZ", 1024 * c, 1024 * c + 1024, t), ind(t_("geno_s"), t_("boff", 64 * c, 64 * c + 64, t)), AF.Copy)
+            e = VG.get(t, 0) // 16 if c == 3 else 0
+            act(t_("CZ", 1024 * c, 1024 * c + 1024 - 16 * e, t), ind(t_("geno_s"), t_("boff", 64 * c, 64 * c + 64 - e, t)), AF.Copy)
+            if e:
+                cp(t_("CZ", 4096 - 16 * e, 4096, t), ind(t_("geno_s"), t_("boff", 256 - e, 256, t)))
         keep(t_("geno_s", t, 4096, step=16), z)
         if t == STEPS - 1:
             store("sg", T.ygeno[:], t_("geno_s"))
-        tt(t_("db", c=t), ind(t_("btab", 0, 1024), vl), t_("NEW", c=t), OP.subtract)
+        act(t_("bg", c=t), ind(t_("btab", 0, 1024), vl), AF.Copy)
         act(t_("qg", c=t), ind(t_("qtab", 0, 1024), vl), AF.Copy)
-        act(t_("ig", c=t), ind(t_("itab", 0, 1024), vl), AF.Copy)
-        act(t_("im1", c=t), t_("ig", c=t), AF.Identity, bias=-1.0)
-        ts(t_("fl", c=t), t_("qg", c=t), float(t + 1), None, OP.is_ge)
-        tt(t_("gt", c=t), t_("ig", c=t), p_(0, 0, 256), OP.is_lt)
+        act(t_("im1", c=t), ind(t_("itab", 0, 1024), vl), AF.Identity, bias=-1.0)
+        act(t_("fl", c=t), t_("qg", c=t), AF.Sigmoid, bias=-200.0 * t - 100.0, scale=200.0)
+        tt(t_("gt", c=t), t_("im1", c=t), p_(0, 256, 512), OP.is_lt)
         gk = ("key", t)
         mm(p_(1, 0, 256), t_("I"), t_("C16"), True, False, gk, "first")
         mm(p_(2, 0, 256), t_("I"), t_("C16"), True, False)
@@ -463,12 +524,18 @@ def rank_program(g, core, T, topo):
         tt(t_("awsl", 0, 256, t), ind(t_("thr", c=t), t_("bc")), t_("keys", c=t), OP.is_gt)
         for x in (2, 3, 0, 1):
             mm(p_(4, 128 * x, 128 * x + 128), t_("awsl", 128 * x, 128 * x + 128, t), t_("I"), True, True)
-        tt(t_("tb"), p_(4, 256, 512), t_("db", c=t), OP.mult)
-        tt(ind(t_("btab"), wl), t_("tb"), t_("NEW", c=t), OP.add)
+        mm(p_(1, 256, 512), t_("I"), t_("row16"), True, False)
+        for h in range(2):
+            w = t_("awsl", 256 + 128 * h, 384 + 128 * h, t)
+            if t:
+                mm(p_(1, 256 + 128 * h, 384 + 128 * h), w, t_("nIt", c=t), False, False)
+            mm(p_(1, 256 + 128 * h, 384 + 128 * h), w, t_("nD", c=h), False, h == 1)
+        act(t_("ns"), p_(1, 256, 512), AF.Identity, bias=float(t))
+        tt(t_("tb"), p_(4, 256, 512), t_("bg", c=t), OP.mult)
+        tt(ind(t_("btab"), wl), t_("tb"), t_("ns"), OP.add)
         tt(t_("t1"), p_(4, 0, 256), t_("qg", c=t), OP.mult)
-        act(t_("t2"), t_("t1"), AF.Identity, bias=-float(8 + t))
-        tt(t_("t3"), p_(4, 256, 512), t_("t2"), OP.mult)
-        ts(ind(t_("qtab"), wl), t_("t3"), 1.0, float(8 + t), OP.mult, OP.add)
+        act(t_("t2"), p_(4, 256, 512), AF.Identity, bias=float(8 + t), scale=-float(8 + t))
+        tt(ind(t_("qtab"), wl), t_("t1"), t_("t2"), OP.max)
         for j in range(8):
             act(t_("Y", 32 * j, 32 * j + 32, t), t_("KM", c=t), AF.Copy, scale=t_("Gmf", j, j + 1))
         for k in range(8):
@@ -481,6 +548,9 @@ def rank_program(g, core, T, topo):
             cp(t_("al", 8 * x, 8 * x + 8, t), t_("of", x, 32, 0, 4))
         act(t_("CZ", 4368, 4880, t), ind(t_("CZ", 0, 4368, t), t_("al", c=t)), AF.Copy)
         a12, a1, a2 = t_("CZ", 4368, 4880, t), t_("CZ", 4368, 4624, t), t_("CZ", 4624, 4880, t)
+        for k in (768, 1536):
+            keep(t_("CZ", 4112 + k, 4368 + k, t), z)
+            keep(t_("CZ", 4368 + k, 4880 + k, t), a12)
         mm(p_(6, 0, 512), t_("nI"), a12, True, False)
         mm(p_(6, 0, 256), t_("I"), z, False, False)
         mm(p_(6, 256, 512), t_("I"), z, False, True)
@@ -488,11 +558,15 @@ def rank_program(g, core, T, topo):
         mm(p_(7, 0, 256), t_("nI"), a2, False, True)
         act(t_("SG", 0, 512), p_(6, 0, 512), AF.Sign, bias=-0.5, scale=-1.0)
         act(t_("SG", 512, 1024), p_(6, 0, 512), AF.Sign, bias=-0.5)
-        act(t_("SG", 1024, 1280), p_(7, 0, 256), AF.Sign, bias=-0.5, scale=-1.0)
-        act(t_("SG", 1280, 1536), p_(7, 0, 256), AF.Sign, bias=-0.5)
+        if t + 1 < STEPS:
+            act(t_("SG", 1024, 1280), p_(7, 0, 256), AF.Sign, bias=-0.5, scale=-1.0)
+            act(t_("SG", 1280, 1536), p_(7, 0, 256), AF.Sign, bias=-0.5)
+        else:
+            ts(t_("SG", 1024, 1280), p_(7, 0, 256), 0.0, -0.5, OP.is_lt, OP.add)
+            ts(t_("SG", 1280, 1536), p_(7, 0, 256), 0.0, -0.5, OP.is_gt, OP.add)
         for r in range(16):
             mm(p_(5, 64, 160), t_("EB", 15 - r, 143 - r), t_("SG", r, 1536, 0, 16), r == 0, r == 15)
-        ts(t_("TH"), p_(5, 64, 160), 2.0, 1024.0, OP.is_ge, OP.mult)
+        ts(t_("TH"), p_(5, 64, 160), 1.0, 768.0, OP.is_ge, OP.mult)
         tt(t_("KK", 0, 16), t_("TH", 0, 16), t_("TH", 16, 32), OP.add)
         tt(t_("KK", 16, 48), t_("TH", 32, 64), t_("TH", 64, 96), OP.add)
         tt(t_("KL"), t_("KK"), t_("C48"), OP.add)
@@ -502,10 +576,8 @@ def rank_program(g, core, T, topo):
         tt(t_("FM", 0, 16), t_("mna"), k2, OP.min)
         tt(t_("tta"), t_("mxa"), k2, OP.min)
         tt(t_("FM", 16, 32), t_("mna"), t_("tta"), OP.max)
-        cp(t_("FI"), t_("FM"))
-        ts(t_("FA"), t_("FI"), 1023, None, OP.bitwise_and)
-        cp(t_("fml", c=t), t_("FA"))
-        win = t_("CZ", 4112, 4880, t)
+        cp(t_("fml", c=t), t_("FM"))
+        win = t_("CZ", 4112, 6416, t)
         if t + 2 < STEPS:
             f, m = t_("fmb", 0, 256), t_("fmb", 256, 512)
             act(t_("fmb"), ind(win, t_("fml", c=t)), AF.Copy)
@@ -550,8 +622,7 @@ def rank_program(g, core, T, topo):
     prio = [0.0] * n
     for j in range(n - 1, -1, -1):
         prio[j] = max([lag.get(j, ops[j]["cost"])] + [l + prio[i] for i, l in succ[j]])
-    order = list_schedule(n, [o["q"] for o in ops], [o["cost"] for o in ops], succ, [len(e) for e in edges],
-                          [prio[i] + BIAS.get(ops[i]["tag"], 0.0) for i in range(n)])[0]
+    order = best_order(n, [o["q"] for o in ops], [o["cost"] for o in ops], succ, [prio[i] + BIAS.get(ops[i]["tag"], 0.0) for i in range(n)], 3)[0]
 
     eng = {"v": g.vector, "s": g.scalar, "p": g.tensor, "g": g, "y": g.sync}
     total = {}

from concourse.mybir import dt, AluOpType, AxisListType, ActivationFunctionType

OP = AluOpType
AF = ActivationFunctionType
BIG = 1048576.0
STEPS = 6
TILES = {
    "bt": (256, "bfloat16", 1), "geno_s": (4096, "bfloat16", 1), "bk": (1024, "int32", 1), "im0": (1024, "bfloat16", 1),
    "wti": (1, "int32", 1), "btab": (1280, "float32", 1), "qtab": (1280, "float32", 1), "itab": (1280, "float32", 1),
    "cb": (256, "bfloat16", 4),
    "CZ": (6416, "bfloat16", 6), "mx": (4096, "bfloat16", 2),
    "bki": (1024, "int32", 1), "qki": (1024, "int32", 1),
    "yb": (1024, "float32", 1), "yi": (1024, "bfloat16", 1),
    "pI": (8, "int32", 1), "pM": (8, "int32", 1), "pG": (8, "int32", 1), "pf": (32, "float32", 1), "wf": (16, "float32", 1), "wi2": (16, "int32", 1),
    "ic": (256, "float32", 1), "icg": (128, "float32", 1), "ir": (256, "float32", 1),
    "I": (128, "bfloat16", 1), "nI": (128, "bfloat16", 1), "IB": (128, "bfloat16", 1), "I16": (128, "bfloat16", 1), "Is": (128, "bfloat16", 1),
    "row16": (256, "bfloat16", 1), "nD": (128, "bfloat16", 2), "nIt": (128, "bfloat16", 6), "lc": (16, "float32", 1),
    "Gf": (128, "bfloat16", 1), "Gs": (128, "float32", 1), "SC": (128, "float32", 1), "wSh": (128, "bfloat16", 1), "wSl": (128, "bfloat16", 1),
    "Gm": (16, "bfloat16", 1), "Gmf": (8, "float32", 1), "G64": (16, "bfloat16", 1), "G32": (16, "bfloat16", 1),
    "EB": (144, "bfloat16", 1), "wE": (144, "float16", 1), "ww": (32, "float32", 1), "RB": (240, "bfloat16", 1),
    "C16": (256, "bfloat16", 1), "ones": (128, "bfloat16", 1), "kidx": (256, "int32", 1),
    "bci": (16, "int32", 1), "bc": (16, "uint16", 1), "lnO": (16, "float32", 1), "lnD": (16, "float32", 1), "LR": (2048, "float16", 1), "Mk": (256, "bfloat16", 1), "m1": (256, "bfloat16", 1), "C48": (48, "float32", 1),
    "ln32": (32, "float32", 1), "ls32": (32, "float32", 1), "tp32": (32, "float32", 1), "ba32": (32, "float32", 1), "sp32": (32, "float32", 1),
    "ui": (16, "int32", 2), "u": (16, "int32", 2), "sq": (16, "int32", 2), "sh": (16, "int32", 2), "u37": (16, "int32", 2), "base": (16, "int32", 2),
    "vb": (16, "int32", 2), "vh": (16, "float16", 2), "bb": (16, "float32", 2), "cs": (16, "float32", 2), "ri": (16, "int32", 2), "fr": (16, "float32", 2),
    "junk": (256, "bfloat16", 8), "c1": (16, "float32", 2), "c2": (16, "float32", 2),
    "bti": (256, "int32", 2), "bit": (256, "int32", 2),
    "vA": (16, "int32", 2), "v": (16, "int32", 2), "vl": (16, "uint16", 2), "dup": (16, "float32", 2), "dv": (16, "float32", 2), "dw": (16, "float32", 2),
    "wo": (16, "float32", 2), "wl": (16, "uint16", 2),
    "boff": (256, "uint16", 2), "bg": (256, "float32", 2), "ns": (256, "float32", 1), "qg": (256, "bfloat16", 2), "im1": (256, "float32", 2),
    "fl": (256, "bfloat16", 2), "gt": (256, "bfloat16", 2), "qks": (128, "float32", 2), "q1": (128, "float32", 2), "q2": (64, "float32", 2), "q3": (32, "float32", 2),
    "m0": (16, "float32", 2), "n1": (32, "float32", 2), "nsB": (32, "float32", 2), "sk": (16, "float32", 2), "ac": (16, "bfloat16", 2), "A": (8, "float32", 2),
    "keys": (256, "float32", 2), "h1": (128, "float32", 1), "l1": (128, "float32", 1), "h2": (64, "float32", 1), "mn2": (64, "float32", 1), "ml2": (64, "float32", 1), "l2": (64, "float32", 1),
    "h3": (32, "float32", 1), "mn3": (32, "float32", 1), "ml3": (32, "float32", 1), "l3": (32, "float32", 1), "mn4": (16, "float32", 1), "ml4": (16, "float32", 1),
    "HL": (32, "float32", 2), "flg": (32, "float32", 2), "HI": (32, "int32", 2), "HA": (32, "int32", 2), "KM": (32, "float32", 2), "thr": (16, "float32", 2),
    "kx": (16, "float32", 2), "sm": (16, "float32", 2), "si": (16, "int32", 2), "sl": (16, "int32", 2), "awsl": (512, "bfloat16", 2),
    "tb": (256, "float32", 1), "t1": (256, "float32", 1), "t2": (256, "float32", 1),
    "Y": (256, "bfloat16", 2), "mz": (32, "float32", 1), "tm": (32, "float32", 1), "bm": (32, "float32", 1), "of": (32, "float32", 1), "al": (32, "uint16", 2),
    "SG": (1536, "bfloat16", 1), "TH": (96, "float32", 1), "KK": (48, "float32", 1), "KL": (48, "float32", 1), "mna": (16, "float32", 1), "mxa": (16, "float32", 1), "tta": (16, "float32", 1),
    "FM": (32, "float32", 1), "FI": (32, "int32", 1), "FA": (32, "int32", 1), "fml": (32, "uint16", 2), "fmb": (512, "bfloat16", 1), "ff": (256, "float32", 1), "tX": (256, "bfloat16", 1),
}
BYTES = {"float32": 4, "int32": 4, "bfloat16": 2, "uint16": 2, "float16": 2}
PLACE = {}
_size = {d: 0 for d in BYTES}
for _n, (_w, _d, _c) in TILES.items():
    _p = (_w + 15) // 16 * 16
    PLACE[_n] = (_size[_d], _p)
    _size[_d] += _p * _c
BUF = {"float32": "bigf", "int32": "bigi", "bfloat16": "bigb", "uint16": "bigu", "float16": "bigh"}
SCRATCH = {BUF[_d]: ("sbuf", [128, _size[_d]], _d) for _d in BYTES}
for _k in range(8):
    SCRATCH["P%d" % _k] = ("psum", [128, 512], "float32")
LOADS = ["bites", "next", "wt", "bank", "immun", "geno"]
STORES = ["sg", "sb0", "sb1", "si0", "si1"]
SEMAPHORES = ["qv", "qs", "qp", "qg", "rl"] + ["arr%d" % t for t in range(1, STEPS)] + ["ld_" + n for n in LOADS] + ["st_" + n for n in STORES]


BIAS = {'C48': -8, 'CZ': 2, 'G64': 14, 'Gm': 9, 'Gs': 10, 'I': 20, 'KK': -9, 'LR': -1, 'P1fl': 3, 'P2fl': 8, 'P2ones': -14, 'P3I': -1, 'P4awsl': -1,
        'P4qtab': 3, 'P6I': 2, 'P6nI': -7, 'SC': 6, 'ac': 12, 'al': -3, 'ba32': -6, 'base': 3, 'bb': 5, 'bci': 17, 'bk': -13, 'btab': 3, 'bti': -4,
        'c1': 4, 'cs': -12, 'flg': 13, 'geno_s': -27, 'ic': -10, 'im0': 3, 'ir': -2, 'itab': -1, 'keys': 11, 'kidx': -3, 'lnD': -6, 'lnO': 2,
        'ls32': 7, 'm0': -1, 'm1': 3, 'ml4': -4, 'mn4': -6, 'n1': 11, 'nI': -11, 'ns': 1, 'of': -4, 'outsb1': 1, 'outsi1': 6, 'pG': 3, 'qki': -8,
        'qtab': -5, 'sh': 1, 'sk': 3, 'sm': -1, 'sp32': 9, 't1': 8, 'thr': -6, 'tp32': -1, 'v': 31, 'vh': 4, 'vl': 19, 'wi2': 1, 'wo': -4, 'wti': -7}
COST = {"us": 0.00083 * 1.25, "ps": 0.00071 * 1.25, "gather": 1.56, "scatter": 3.8, "wake": 0.08, "link": 4.0}
LOOK = 0.3
VG = {t: 512 for t in range(STEPS)}


def list_schedule(n, que, cost, succ, need, prio):
    need = list(need)
    when = [0.0] * n
    free, ready, nxt = {}, {}, {}
    order = []
    for i in range(n):
        if need[i] == 0:
            ready.setdefault(que[i], []).append(i)
    dirty = set(ready)
    end = 0.0
    while len(order) < n:
        for q in dirty:
            lst = ready.get(q)
            if not lst:
                nxt.pop(q, None)
                continue
            f = free.get(q, 0.0)
            st = max(f, min(when[i] for i in lst))
            c = -1
            for i in lst:
                if when[i] <= st + 1e-9 and (c < 0 or prio[i] > prio[c]):
                    c = i
            if cost[c] > LOOK:
                lim = st + min(LOOK, 0.5 * cost[c])
                b = c
                for i in lst:
                    if when[i] <= lim and prio[i] > prio[b]:
                        b = i
                c = b
            nxt[q] = (max(st, when[c]), c)
        q = min(nxt, key=lambda x: nxt[x][0])
        st, c = nxt[q]
        ready[q].remove(c)
        order.append(c)
        free[q] = st + cost[c] if q != "n" else 0.0
        end = max(end, st + cost[c])
        dirty = {q}
        for i, l in succ[c]:
            need[i] -= 1
            if st + l > when[i]:
                when[i] = st + l
            if need[i] == 0:
                ready.setdefault(que[i], []).append(i)
                dirty.add(que[i])
    return order, end


def best_order(n, que, cost, succ, prio, rounds=2):
    need = [0] * n
    for j in range(n):
        for i, l in succ[j]:
            need[i] += 1
    back = [[] for _ in range(n)]
    for j in range(n):
        for i, l in succ[j]:
            back[i].append((j, max(0.0, cost[i] + l - cost[j])))
    bneed = [len(x) for x in succ]

    def starts(order, follow):
        at, when, free = [0.0] * n, [0.0] * n, {}
        for i in order:
            st = when[i]
            if que[i] != "n":
                st = max(st, free.get(que[i], 0.0))
                free[que[i]] = st + cost[i]
            at[i] = st
            for k, l in follow[i]:
                if st + l > when[k]:
                    when[k] = st + l
        return at
    best = None
    for k in range(rounds):
        order, end = list_schedule(n, que, cost, succ, need, prio)
        if best is None or end < best[1]:
            best = (order, end)
        if k + 1 < rounds:
            at = starts(order, succ)
            rev = list_schedule(n, que, cost, back, bneed, [at[i] + cost[i] for i in range(n)])[0]
            at = starts(rev, back)
            prio = [at[i] + cost[i] for i in range(n)]
    return best


def rank_program(g, core, T, topo):
    rank = T.rank_of(core)
    if rank is None:
        return
    n_ranks = len(T.cores)
    ops = []
    last = {}
    edges = []
    US, PS = COST["us"], COST["ps"]

    def t_(name, a=0, b=None, c=0, step=1):
        w, d, copies = TILES[name]
        if b is None:
            b = w
        off, p = PLACE[name]
        off += p * (c % copies)
        ap = T[BUF[d]][:, off + a:off + b:step] if step != 1 else T[BUF[d]][:, off + a:off + b]
        return {"ap": ap, "rg": [(BUF[d], off + a, off + b)], "n": (b - a + step - 1) // step, "by": BYTES[d], "ps": False, "ind": False}

    def p_(k, a, b, step=1, grp=None):
        ap = T["P%d" % k][:, a:b:step] if step != 1 else T["P%d" % k][:, a:b]
        return {"ap": ap, "rg": [("P%d" % k, 0, 512)], "n": (b - a + step - 1) // step, "by": 4, "ps": True, "ind": False, "grp": grp}

    def ind(win, off):
        return {"ap": win["ap"].indirect(off["ap"]), "rg": win["rg"] + off["rg"], "win": win["rg"], "off": off["rg"], "n": 16 * off["n"], "by": win["by"], "ps": False, "ind": True}

    starts = {d: sorted((PLACE[x][0], x) for x in TILES if TILES[x][1] == d) for d in BUF}
    dtype_of = {BUF[d]: d for d in BUF}

    def name_of(region):
        if region[0] not in dtype_of:
            return region[0]
        return [x for o, x in starts[dtype_of[region[0]]] if o <= region[1]][-1]

    def add(q, cost, emit, R, W, sem, inc, grp=None, role=None, extra=()):
        i = len(ops)
        ed = {}
        acc = [(r, False) for r in R] + [(r, True) for r in W]
        for (buf, a, b), wr in acc:
            ps = buf.startswith("P") and len(buf) == 2
            for (a2, b2, j, wr2, q2, grp2, role2) in last.get(buf, []):
                if a2 >= b or b2 <= a or j == i:
                    continue
                if ps:
                    if q2 == q:
                        if q == "p" and not (grp is not None and grp == grp2 and role == "mid" and role2 == "mid"):
                            ed.setdefault(j, 0)
                    else:
                        ed[j] = 1
                elif wr or wr2:
                    ed[j] = 1
        for j in extra:
            ed[j] = 1
        for (buf, a, b), wr in acc:
            ps = buf.startswith("P") and len(buf) == 2
            lst = last.setdefault(buf, [])
            if wr and not ps:
                lst[:] = [x for x in lst if not (x[0] >= a and x[1] <= b and x[2] != i)]
            lst.append((a, b, i, wr, q, grp, role))
            if ps and len(lst) > 200:
                del lst[:80]
        tag = name_of(W[0]) if W else q
        if tag[0] == "P" and R:
            tag += name_of(R[0])
        ops.append({"q": q, "cost": cost, "emit": emit, "sem": sem, "inc": inc, "tag": tag})
        edges.append(ed)
        return i

    def rgs(*xs):
        out = []
        for x in xs:
            if isinstance(x, dict):
                out += x["rg"]
        return out

    def raw(x):
        return x["ap"] if isinstance(x, dict) else x

    def vcost(n, mode, xs):
        if any(x["ind"] for x in xs[1:]):
            return 0.05 + n * COST["gather"] * US
        if xs[0]["ind"]:
            return 0.05 + n * COST["scatter"] * US
        if mode == "tt":
            c = n * (1 if any(x["ps"] for x in xs) else 2)
        else:
            c = n * (0.5 if all(x["by"] == 2 for x in xs) else 1)
        return max(64, c) * US

    def outrg(out):
        return (out["off"], out["win"]) if out["ind"] else ([], out["rg"])

    def tt(out, a, b, op):
        r, w = outrg(out)
        n = out["n"]
        return add("v", vcost(n, "tt", [out, a, b]), lambda: g.vector.tensor_tensor(raw(out), raw(a), raw(b), op), rgs(a, b) + r, w, "qv", 1)

    def ts(out, a, s1, s2, o1, o2=None):
        r, w = outrg(out)
        f = (lambda: g.vector.tensor_scalar(raw(out), raw(a), raw(s1), raw(s2), o1)) if o2 is None else (lambda: g.vector.tensor_scalar(raw(out), raw(a), raw(s1), raw(s2), o1, o2))
        return add("v", vcost(out["n"], "ts", [out, a]), f, rgs(a, s1, s2) + r, w, "qv", 1)

    def cp(out, a):
        r, w = outrg(out)
        return add("v", vcost(out["n"], "ts", [out, a]), lambda: g.vector.tensor_copy(raw(out), raw(a)), rgs(a) + r, w, "qv", 1)

    def ms(out, val):
        return add("v", max(64, out["n"]) * US, lambda: g.vector.memset(raw(out), val), [], out["rg"], "qv", 1)

    def red(out, a):
        return add("v", 64 * US, lambda: g.vector.tensor_reduce(raw(out), raw(a), AxisListType.X, OP.add), rgs(a), out["rg"], "qv", 1)

    def act(out, a, fn, bias=0.0, scale=1.0, acc=None):
        c = 0.065 + a["n"] * COST["gather"] * US if a["ind"] else max(64, a["n"]) * US
        w = out["rg"] + (acc["rg"] if acc else [])
        if acc:
            c += 0.02
            f = lambda: g.scalar.activation(raw(out), raw(a), fn, bias=raw(bias), scale=scale, accum_out=raw(acc))
        elif isinstance(bias, float) and bias == 0.0:
            f = (lambda: g.scalar.activation(raw(out), raw(a), fn, scale=raw(scale))) if scale != 1.0 else (lambda: g.scalar.activation(raw(out), raw(a), fn))
        else:
            f = lambda: g.scalar.activation(raw(out), raw(a), fn, bias=raw(bias), scale=scale)
        return add("s", c, f, rgs(a, bias, scale), w, "qs", 1)

    def mm(out, lhsT, rhs, start, stop, grp=None, role=None, f32=False):
        c = max(64, rhs["n"]) * PS * (4 if f32 else 1)
        return add("p", c, lambda: g.tensor.matmul(raw(out), raw(lhsT), raw(rhs), start, stop), rgs(lhsT, rhs), out["rg"], "qp", 1, grp=grp, role=role)

    def iota(out, pattern, base=0, cm=0):
        small = out["flt"] if "flt" in out else False
        def f():
            if small:
                return g.iota(raw(out), pattern, base, cm, allow_small_or_imprecise_dtypes=True)
            return g.iota(raw(out), pattern, base, cm)
        return add("g", 0.13 + 2 * out["n"] * US, f, [], out["rg"], "qg", 1)

    def keep(out, a):
        return add("g", 0.17 + 2 * out["n"] * US, lambda: g.affine_select(raw(out), raw(a), [[0, out["n"]]], OP.is_ge, 0.0, 0, 0), rgs(a), out["rg"], "qg", 1)

    def flt(x):
        x["flt"] = True
        return x

    def load(name, out, q="y"):
        eng = g.sync if q == "y" else g.scalar
        src = T.bites[:, 0:256] if name == "bites" else T.bites[:, 256:512] if name == "next" else T[name][:]
        return add(q, 0.1, lambda: eng.dma_start(raw(out), src), [], out["rg"], "ld_" + name, 16)

    def store(tag, dst, src, q="y"):
        eng = g.sync if q == "y" else g.scalar
        return add(q, 0.1, lambda: eng.dma_start(dst, raw(src)), src["rg"], [("out" + tag, 0, 1)], "st_" + tag, 16)

    lag = {}

    for name, dst, tm in (("bites", t_("CZ", 4112, 4368, 0), 2.6), ("wt", t_("wti"), 2.5), ("bank", t_("bk"), 4.5), ("immun", t_("im0"), 5.0), ("next", t_("bt"), 4.0), ("geno", t_("geno_s"), 7.0)):
        i = load(name, dst, "s" if name in ("wt", "immun", "next") else "y")
        lag[i] = tm

    def send(src, t, dst_rank):
        dst = T.cores[dst_rank]
        rid, pid, _se = topo.addr(dst)
        m = topo.mask(core, dst)
        eng = len(topo.engines(core, dst))
        out = t_("CZ", 4112, 4368, t)
        def f():
            return g.remote_dma(raw(out), raw(src), T.sem["arr%d" % t], T.sem.rl, pid, rid, m)
        i = add("g", 0.3, f, src["rg"], [], None, 0)
        ops[i]["remote"] = eng
        lag[i] = 0.3
        j = add("n", 0.0, None, [], out["rg"], "arr%d" % t, eng)
        ops[j]["proxy"] = i
        lag[j] = 0.0
        return i

    iota(t_("pI", 0, 1), [[0, 1]], 0, 1)
    iota(flt(t_("ic", 0, 128)), [[1, 128]])
    iota(flt(t_("icg")), [[1, 8], [0, 16]])
    iota(flt(t_("ir")), [[0, 16], [1, 16]])
    iota(t_("bci"), [[1, 16]])
    iota(t_("kidx"), [[0, 16], [1, 16]])
    iota(flt(t_("lnO")), [[16, 16]])
    iota(flt(t_("ln32")), [[16, 8], [0, 2], [128, 2]])
    iota(flt(t_("ls32")), [[0, 8], [1, 2], [0, 2]])
    send(t_("bt"), 1, (rank + 1) % n_ranks)
    ts(t_("pM", 0, 1), t_("pI", 0, 1), 15, None, OP.bitwise_and)
    ts(t_("pG", 0, 1), t_("pI", 0, 1), 4, None, OP.arith_shift_right)
    P, PM, PG = t_("pf", 0, 1), t_("pf", 8, 9), t_("pf", 16, 17)
    cp(P, t_("pI", 0, 1))
    cp(PM, t_("pM", 0, 1))
    cp(PG, t_("pG", 0, 1))
    ts(t_("Gmf"), t_("ic", 0, 8), PG, None, OP.is_equal)
    ms(t_("EB"), 0.0)
    cp(t_("EB", 15, 128, step=16), t_("Gmf"))
    ts(t_("wi2", 0, 1), t_("wti"), 4032, None, OP.bitwise_and)
    ts(t_("wi2", 8, 9), t_("wti"), 63, None, OP.bitwise_and)
    WH, WL = t_("wf", 0, 1), t_("wf", 8, 9)
    cp(WH, t_("wi2", 0, 1))
    cp(WL, t_("wi2", 8, 9))
    WF, WG, WS = t_("ww", 0, 1), t_("ww", 8, 9), t_("ww", 16, 17)
    cp(WF, t_("wti"))
    ts(WG, WF, 2047.5, -4096.0, OP.is_gt, OP.mult)
    tt(WS, WF, WG, OP.add)
    ts(t_("wE"), t_("EB"), WS, None, OP.mult)
    ts(t_("lnO"), t_("lnO"), PM, None, OP.add)
    ts(t_("lnD"), t_("lnO"), 1024.0, None, OP.add)
    cp(t_("bc"), t_("bci"))
    ts(t_("Gf"), t_("icg"), PG, None, OP.is_equal)
    ts(t_("I"), t_("ic", 0, 128), P, None, OP.is_equal)
    ts(t_("bki"), t_("bk"), 4095, None, OP.bitwise_and)
    cp(t_("btab", 0, 1024), t_("bki"))
    ts(t_("qki"), t_("bk"), 12, None, OP.arith_shift_right)
    cp(t_("qtab", 0, 1024), t_("qki"))
    act(t_("itab", 0, 1024), t_("im0"), AF.Copy)
    cp(t_("Gm", 0, 8), t_("Gmf"))
    ts(t_("G64", 0, 8), t_("Gmf"), 1024.0, None, OP.mult)
    ts(t_("G32", 0, 8), t_("Gmf"), -512.0, None, OP.mult)
    ts(t_("nI"), t_("I"), -1.0, None, OP.mult)
    ts(t_("IB"), t_("I"), BIG, None, OP.mult)
    ts(t_("I16"), t_("I"), -16.0, None, OP.mult)
    ts(t_("Is"), t_("I"), 1.0 / 128, None, OP.mult)
    ts(t_("C16"), t_("ir"), -1.0, 256.0, OP.mult, OP.add)
    ms(t_("ones"), 1.0)
    ms(t_("RB"), 0.0)
    ts(t_("RB", 112, 128), t_("ir", 0, 16), PM, None, OP.is_equal)
    for r in range(16):
        ts(t_("LR", 128 * r, 128 * r + 128), t_("Gf"), t_("RB", 112 + r, 113 + r), None, OP.mult)
    iota(flt(t_("row16")), [[16, 256]])
    for h in range(2):
        ts(t_("lc", 8 * h, 8 * h + 1), P, -16.0, -2048.0 * h, OP.mult, OP.add)
        ts(t_("nD", c=h), t_("I"), t_("lc", 8 * h, 8 * h + 1), None, OP.mult)
    for t in range(1, STEPS):
        ts(t_("nIt", c=t), t_("I"), float(-t), None, OP.mult)
    ts(t_("Mk"), t_("ir"), PM, 2048.0, OP.is_ge, OP.mult)
    for c in range(2):
        ms(t_("c1", 0, 1, c), 0.0)
    ms(t_("m1"), -1.0)
    for c in range(STEPS):
        ms(t_("CZ", 4096, 4112, c), 0.0)
    for s in range(8):
        ms(t_("SC", s, 128, step=8), float(1 << (7 - s)))
    tt(t_("Gs"), t_("Gf"), t_("SC"), OP.mult)
    ts(t_("wSh"), t_("Gs"), WH, None, OP.mult)
    ts(t_("wSl"), t_("Gs"), WL, None, OP.mult)
    ts(t_("ln32"), t_("ln32"), PM, None, OP.add)
    ts(t_("ba32"), t_("ln32"), 16.0, 256.0, OP.mult, OP.add)
    ts(t_("tp32"), t_("ln32"), 16.0, None, OP.add)
    tt(t_("tp32"), t_("tp32"), t_("ls32"), OP.mult)
    ts(t_("sp32"), t_("ln32"), -15.0, 3856.0, OP.mult, OP.add)
    tt(t_("sp32"), t_("sp32"), t_("tp32"), OP.subtract)
    for k in range(3):
        ts(t_("C48", 16 * k, 16 * k + 16), t_("lnO"), 256.0 * k, None, OP.add)

    def zt(t, a=0, b=256, step=1):
        return t_("CZ", 4112 + a, 4112 + b, t, step)

    def early(t):
        z = zt(t)
        for r in range(16):
            mm(p_(2, 320, 336), t_("wE", 15 - r, 143 - r), zt(t, r, 256, 16), r == 0, r == 15)
        cp(t_("ui", c=t), p_(2, 320, 336))
        ts(t_("u", c=t), t_("ui", c=t), 4095, None, OP.bitwise_and)
        tt(t_("sq", c=t), t_("u", c=t), t_("u", c=t), OP.mult)
        ts(t_("u37", c=t), t_("u", c=t), 37.0, None, OP.mult)
        ts(t_("sh", c=t), t_("sq", c=t), 5, None, OP.arith_shift_right)
        tt(t_("base", c=t), t_("sh", c=t), t_("u37", c=t), OP.add)
        ts(t_("vb", c=t), t_("base", c=t), 1023, None, OP.bitwise_and)
        cp(t_("vh", c=t), t_("vb", c=t))
        for b in (256, 0):
            if b == 0:
                mm(p_(3, 0, 256), t_("I"), t_("Mk"), True, False)
            for r in range(16):
                mm(p_(3, b + r, b + 256, 16), t_("LR", 128 * r, 128 * r + 128), t_("vh", c=t), b == 256, b == 256 or r == 15)
        ts(t_("bb", c=t), t_("vb", c=t), -32.0, -5.7, OP.mult, OP.add)
        for j in range(15, -1, -1):
            if j:
                act(t_("junk", 0, 16 * j, 2 * j), p_(3, 256, 256 + 16 * j), AF.Sigmoid, bias=t_("bb", j, j + 1, t), scale=32.0, acc=t_("c1", j, j + 1, t))
            act(t_("junk", 0, 16, 2 * j + 1), p_(3, 16 * j, 16 * j + 16), AF.Sigmoid, bias=t_("bb", j, j + 1, t), scale=32.0, acc=t_("c2", j, j + 1, t))
        tt(t_("cs", c=t), t_("c1", c=t), t_("c2", c=t), OP.add)
        ts(t_("ri", c=t), t_("cs", c=t), -0.45, None, OP.add)
        tt(t_("fr", c=t), t_("cs", c=t), t_("ri", c=t), OP.subtract)
        ts(t_("dup", c=t), t_("fr", c=t), 0.0017, None, OP.is_gt)

    def step(t):
        if t == 0:
            early(0)
        z = zt(t)
        mm(p_(0, 0, 256), t_("I"), z, True, True)
        mm(p_(0, 256, 512), t_("I"), z, True, False)
        mm(p_(0, 256, 512), t_("I"), t_("m1"), False, True)
        if t:
            ts(t_("vA", c=t), t_("base", c=t), t_("A", 0, 1, t - 1), None, OP.add)
            ts(t_("v", c=t), t_("vA", c=t), 1023, None, OP.bitwise_and)
        else:
            ts(t_("v", c=t), t_("base", c=t), 1023, None, OP.bitwise_and)
        cp(t_("vl", c=t), t_("v", c=t))
        vl, wl = t_("vl", c=t), t_("wl", c=t)
        cp(t_("boff", c=t), ind(t_("btab" if t else "bki", 0, 1024), vl))
        tt(t_("dv", c=t), t_("lnD"), t_("v", c=t), OP.subtract)
        tt(t_("dw", c=t), t_("dv", c=t), t_("dup", c=t), OP.mult)
        tt(t_("wo", c=t), t_("v", c=t), t_("dw", c=t), OP.add)
        cp(wl, t_("wo", c=t))
        for c in range(4):
            e = VG.get(t, 0) // 16 if c == 3 else 0
            act(t_("CZ", 1024 * c, 1024 * c + 1024 - 16 * e, t), ind(t_("geno_s"), t_("boff", 64 * c, 64 * c + 64 - e, t)), AF.Copy)
            if e:
                cp(t_("CZ", 4096 - 16 * e, 4096, t), ind(t_("geno_s"), t_("boff", 256 - e, 256, t)))
        keep(t_("geno_s", t, 4096, step=16), z)
        if t == STEPS - 1:
            store("sg", T.ygeno[:], t_("geno_s"))
        act(t_("bg", c=t), ind(t_("btab", 0, 1024), vl), AF.Copy)
        act(t_("qg", c=t), ind(t_("qtab", 0, 1024), vl), AF.Copy)
        act(t_("im1", c=t), ind(t_("itab", 0, 1024), vl), AF.Identity, bias=-1.0)
        act(t_("fl", c=t), t_("qg", c=t), AF.Sigmoid, bias=-200.0 * t - 100.0, scale=200.0)
        tt(t_("gt", c=t), t_("im1", c=t), p_(0, 256, 512), OP.is_lt)
        gk = ("key", t)
        mm(p_(1, 0, 256), t_("I"), t_("C16"), True, False, gk, "first")
        mm(p_(2, 0, 256), t_("I"), t_("C16"), True, False)
        for h in range(2):
            mm(p_(2, 128 * h, 128 * h + 128), t_("qg", 128 * h, 128 * h + 128, t), t_("I16"), False, h == 1)
        for h in range(2):
            mm(p_(2, 256 + 8 * h, 264 + 8 * h), t_("fl", 128 * h, 128 * h + 128, t), t_("Gm", 0, 8), True, True)
        for h in range(4):
            mm(p_(2, 272 + 8 * h, 280 + 8 * h), t_("gt", 128 * (h % 2), 128 * (h % 2) + 128, t), t_("Gm", 0, 8), True, True)
        act(t_("qks", c=t), p_(2, 1, 256, 2), AF.Copy)
        ts(t_("n1", c=t), p_(2, 272, 304), 9.0, 4194304.0, OP.is_lt, OP.mult)
        ts(t_("nsB", c=t), t_("n1", c=t), BIG, None, OP.max)
        if t + 1 < STEPS:
            ts(t_("sk", c=t), p_(2, 272, 288), 9.0, 2.0, OP.is_ge, OP.mult)
            tt(t_("ac", c=t), t_("sk", c=t), p_(2, 256, 272), OP.min)
            mm(p_(2, 304, 320), t_("ones"), t_("ac", c=t), True, True)
            red(t_("A", 0, 1, t), p_(2, 304, 320))
        tt(t_("q1", c=t), p_(2, 0, 256, 2), t_("qks", c=t), OP.max)
        tt(t_("q2", c=t), t_("q1", 0, 128, t, 2), t_("q1", 1, 128, t, 2), OP.max)
        tt(t_("q3", c=t), t_("q2", 0, 64, t, 2), t_("q2", 1, 64, t, 2), OP.max)
        tt(t_("m0", c=t), t_("q3", 0, 32, t, 2), t_("q3", 1, 32, t, 2), OP.max)
        if t + 1 < STEPS:
            early(t + 1)
        for h in range(2):
            mm(p_(1, 128 * h, 128 * h + 128), t_("fl", 128 * h, 128 * h + 128, t), t_("IB"), False, False, gk, "mid")
            for k in range(16):
                mm(p_(1, 128 * h + k, 128 * h + 128, 16), t_("CZ", 2048 * h + k, 2048 * h + 2048, t, 16), t_("G32", 0, 8), False, False, gk, "mid")
            for k in range(16):
                if h == 0:
                    tt(t_("mx", 128 * k, 128 * k + 128, t), t_("CZ", k, 2048, t, 16), p_(0, 0, 128), OP.max)
                else:
                    for e in range(2):
                        o = 2048 + 128 * k + 64 * e
                        tt(t_("mx", o, o + 64, t), t_("CZ", 2048 + 1024 * e + k, 3072 + 1024 * e, t, 16), p_(0, 128 + 64 * e, 192 + 64 * e), OP.max)
            for k in range(16):
                o = 2048 * h + 128 * k
                end = h == 1 and k == 15
                mm(p_(1, 128 * h + k, 128 * h + 128, 16), t_("mx", o, o + 128, t), t_("G64", 0, 8), False, end, gk, "last" if end else "mid")
        act(t_("keys", c=t), p_(1, 0, 256), AF.Copy)
        ko = t_("keys", 1, 256, t, 2)
        tt(t_("h1"), p_(1, 0, 256, 2), ko, OP.max)
        tt(t_("l1"), p_(1, 0, 256, 2), ko, OP.min)
        for a, b, n in (("1", "2", 128), ("2", "3", 64), ("3", "4", 32)):
            he, ho, le, lo = t_("h" + a, 0, n, step=2), t_("h" + a, 1, n, step=2), t_("l" + a, 0, n, step=2), t_("l" + a, 1, n, step=2)
            tt(t_("HL", 0, 16, t) if b == "4" else t_("h" + b), he, ho, OP.max)
            tt(t_("mn" + b), he, ho, OP.min)
            tt(t_("ml" + b), le, lo, OP.max)
            tt(t_("HL", 16, 32, t) if b == "4" else t_("l" + b), t_("mn" + b), t_("ml" + b), OP.max)
        HL = t_("HL", c=t)
        cp(t_("HI", c=t), HL)
        tt(t_("flg", c=t), HL, t_("nsB", c=t), OP.is_ge)
        ts(t_("HA", c=t), t_("HI", c=t), 511, None, OP.bitwise_and)
        tt(t_("thr", c=t), t_("HL", 16, 32, t), t_("nsB", 0, 16, t), OP.max)
        tt(t_("KM", c=t), t_("HA", c=t), t_("flg", c=t), OP.mult)
        tt(t_("kx", c=t), t_("KM", 0, 16, t), t_("KM", 16, 32, t), OP.max)
        tt(t_("sm", c=t), t_("kx", c=t), t_("m0", c=t), OP.max)
        ts(t_("si", c=t), t_("sm", c=t), -1.0, 256.0, OP.mult, OP.add)
        ts(t_("sl", c=t), t_("si", c=t), 15, None, OP.bitwise_and)
        tt(t_("awsl", 256, 512, t), ind(t_("sl", c=t), t_("bc")), t_("kidx"), OP.not_equal)
        tt(t_("awsl", 0, 256, t), ind(t_("thr", c=t), t_("bc")), t_("keys", c=t), OP.is_gt)
        for x in (2, 3, 0, 1):
            mm(p_(4, 128 * x, 128 * x + 128), t_("awsl", 128 * x, 128 * x + 128, t), t_("I"), True, True)
        mm(p_(1, 256, 512), t_("I"), t_("row16"), True, False)
        for h in range(2):
            w = t_("awsl", 256 + 128 * h, 384 + 128 * h, t)
            if t:
                mm(p_(1, 256 + 128 * h, 384 + 128 * h), w, t_("nIt", c=t), False, False)
            mm(p_(1, 256 + 128 * h, 384 + 128 * h), w, t_("nD", c=h), False, h == 1)
        act(t_("ns"), p_(1, 256, 512), AF.Identity, bias=float(t))
        tt(t_("tb"), p_(4, 256, 512), t_("bg", c=t), OP.mult)
        tt(ind(t_("btab"), wl), t_("tb"), t_("ns"), OP.add)
        tt(t_("t1"), p_(4, 0, 256), t_("qg", c=t), OP.mult)
        act(t_("t2"), p_(4, 256, 512), AF.Identity, bias=float(8 + t), scale=-float(8 + t))
        tt(ind(t_("qtab"), wl), t_("t1"), t_("t2"), OP.max)
        for j in range(8):
            act(t_("Y", 32 * j, 32 * j + 32, t), t_("KM", c=t), AF.Copy, scale=t_("Gmf", j, j + 1))
        for k in range(8):
            mm(p_(5, 0, 32), t_("RB", 112 - 16 * k, 240 - 16 * k), t_("Y", k, 256, t, 8), k == 0, k == 7)
        ts(t_("mz"), p_(5, 0, 32), 0.0, None, OP.is_equal)
        tt(t_("bm"), t_("ba32"), p_(5, 0, 32), OP.subtract)
        tt(t_("tm"), t_("mz"), t_("sp32"), OP.mult)
        tt(t_("of"), t_("tm"), t_("bm"), OP.add)
        for x in range(4):
            cp(t_("al", 8 * x, 8 * x + 8, t), t_("of", x, 32, 0, 4))
        act(t_("CZ", 4368, 4880, t), ind(t_("CZ", 0, 4368, t), t_("al", c=t)), AF.Copy)
        a12, a1, a2 = t_("CZ", 4368, 4880, t), t_("CZ", 4368, 4624, t), t_("CZ", 4624, 4880, t)
        for k in (768, 1536):
            keep(t_("CZ", 4112 + k, 4368 + k, t), z)
            keep(t_("CZ", 4368 + k, 4880 + k, t), a12)
        mm(p_(6, 0, 512), t_("nI"), a12, True, False)
        mm(p_(6, 0, 256), t_("I"), z, False, False)
        mm(p_(6, 256, 512), t_("I"), z, False, True)
        mm(p_(7, 0, 256), t_("I"), a1, True, False)
        mm(p_(7, 0, 256), t_("nI"), a2, False, True)
        act(t_("SG", 0, 512), p_(6, 0, 512), AF.Sign, bias=-0.5, scale=-1.0)
        act(t_("SG", 512, 1024), p_(6, 0, 512), AF.Sign, bias=-0.5)
        if t + 1 < STEPS:
            act(t_("SG", 1024, 1280), p_(7, 0, 256), AF.Sign, bias=-0.5, scale=-1.0)
            act(t_("SG", 1280, 1536), p_(7, 0, 256), AF.Sign, bias=-0.5)
        else:
            ts(t_("SG", 1024, 1280), p_(7, 0, 256), 0.0, -0.5, OP.is_lt, OP.add)
            ts(t_("SG", 1280, 1536), p_(7, 0, 256), 0.0, -0.5, OP.is_gt, OP.add)
        for r in range(16):
            mm(p_(5, 64, 160), t_("EB", 15 - r, 143 - r), t_("SG", r, 1536, 0, 16), r == 0, r == 15)
        ts(t_("TH"), p_(5, 64, 160), 1.0, 768.0, OP.is_ge, OP.mult)
        tt(t_("KK", 0, 16), t_("TH", 0, 16), t_("TH", 16, 32), OP.add)
        tt(t_("KK", 16, 48), t_("TH", 32, 64), t_("TH", 64, 96), OP.add)
        tt(t_("KL"), t_("KK"), t_("C48"), OP.add)
        k0, k1, k2 = t_("KL", 0, 16), t_("KL", 16, 32), t_("KL", 32, 48)
        tt(t_("mna"), k0, k1, OP.min)
        tt(t_("mxa"), k0, k1, OP.max)
        tt(t_("FM", 0, 16), t_("mna"), k2, OP.min)
        tt(t_("tta"), t_("mxa"), k2, OP.min)
        tt(t_("FM", 16, 32), t_("mna"), t_("tta"), OP.max)
        cp(t_("fml", c=t), t_("FM"))
        win = t_("CZ", 4112, 6416, t)
        if t + 2 < STEPS:
            f, m = t_("fmb", 0, 256), t_("fmb", 256, 512)
            act(t_("fmb"), ind(win, t_("fml", c=t)), AF.Copy)
            act(t_("ff"), f, AF.Copy)
            mm(p_(6, 0, 256), t_("I"), f, True, False)
            mm(p_(6, 0, 256), t_("nI"), m, False, True)
            mm(p_(7, 256, 512), t_("wSh"), z, True, False)
            mm(p_(7, 256, 512), t_("wSl"), z, False, True)
            cp(t_("bti", c=t), p_(7, 256, 512))
            ts(t_("bit", c=t), t_("bti", c=t), 128, None, OP.bitwise_and)
            tt(t_("tX"), p_(6, 0, 256), t_("bit", c=t), OP.mult)
            mm(p_(6, 256, 512), t_("I"), m, True, False)
            mm(p_(6, 256, 512), t_("Is"), t_("tX"), False, True)
            act(t_("cb", c=t), p_(6, 256, 512), AF.Copy)
            send(t_("cb", c=t), t + 2, (rank + 2) % n_ranks)
        else:
            act(t_("ff"), ind(win, t_("fml", 0, 16, t)), AF.Copy)
        tt(ind(t_("itab"), wl), t_("im1", c=t), t_("ff"), OP.max)

    for t in range(STEPS):
        step(t)
    act(t_("yi", 0, 512), t_("itab", 0, 512), AF.Copy)
    cp(t_("yi", 512, 1024), t_("itab", 512, 1024))
    for k in range(2):
        store("si%d" % k, T.yimm[:, 512 * k:512 * k + 512], t_("yi", 512 * k, 512 * k + 512))
    for k, b in ((0, 4), (1, 1)):
        act(p_(b, 0, 512), t_("qtab", 512 * k, 512 * k + 512), AF.Copy, scale=4096.0)
        tt(t_("yb", 512 * k, 512 * k + 512), t_("btab", 512 * k, 512 * k + 512), p_(b, 0, 512), OP.add)
        store("sb%d" % k, T.ybank[:, 512 * k:512 * k + 512], t_("yb", 512 * k, 512 * k + 512))

    n = len(ops)
    for i in range(n):
        if "proxy" in ops[i]:
            edges[i][ops[i]["proxy"]] = 0
    succ = [[] for _ in range(n)]
    for i in range(n):
        for j, w in edges[i].items():
            l = lag.get(j, ops[j]["cost"]) + (COST["wake"] if w else 0.0)
            if "proxy" in ops[i]:
                l = COST["link"]
            succ[j].append((i, l))
    prio = [0.0] * n
    for j in range(n - 1, -1, -1):
        prio[j] = max([lag.get(j, ops[j]["cost"])] + [l + prio[i] for i, l in succ[j]])
    order = best_order(n, [o["q"] for o in ops], [o["cost"] for o in ops], succ, [prio[i] + BIAS.get(ops[i]["tag"], 0.0) for i in range(n)], 3)[0]

    eng = {"v": g.vector, "s": g.scalar, "p": g.tensor, "g": g, "y": g.sync}
    total = {}
    at = [None] * n
    know = {q: {} for q in eng}
    snap = [None] * n
    for i in order:
        o = ops[i]
        q = o["q"]
        if q == "n":
            at[i] = (o["sem"], o["inc"])
            snap[i] = {o["sem"]: o["inc"]}
            total[o["sem"]] = o["inc"]
            continue
        k = know[q]
        want = {}
        for j, w in edges[i].items():
            if w and at[j] is not None:
                s, v = at[j]
                if k.get(s, 0) < v and want.get(s, (0, 0))[0] < v:
                    want[s] = (v, j)
        for s in list(want):
            v, j = want[s]
            if any(s2 != s and snap[j2].get(s, 0) >= v for s2, (v2, j2) in want.items()):
                del want[s]
        for s, (v, j) in want.items():
            eng[q].wait_ge(T.sem[s], v)
            for s2, v2 in snap[j].items():
                if k.get(s2, 0) < v2:
                    k[s2] = v2
        ins = o["emit"]()
        if o["sem"] is not None:
            total[o["sem"]] = total.get(o["sem"], 0) + o["inc"]
            ins.then_inc(T.sem[o["sem"]], o["inc"])
            at[i] = (o["sem"], total[o["sem"]])
            snap[i] = dict(k)
            snap[i][o["sem"]] = total[o["sem"]]
        if "remote" in o:
            total["rl"] = total.get("rl", 0) + o["remote"]
    for s in sorted(total):
        if know["g"].get(s, 0) < total[s]:
            g.wait_ge(T.sem[s], total[s])
